import numpy as np
import ml_dtypes


def mxq(x, axis, fmt="e4m3"):
    dtype, down = {"e4m3": (ml_dtypes.float8_e4m3fn, 7), "e5m2": (ml_dtypes.float8_e5m2, 14)}[fmt]
    v = np.moveaxis(np.asarray(x, np.float32).astype(ml_dtypes.bfloat16).astype(np.float64), axis, -1)
    blocks = v.reshape(v.shape[:-1] + (-1, 32))
    amax = np.abs(blocks).max(-1, keepdims=True)
    byte = np.maximum(np.where(amax > 0, np.frexp(amax)[1] - 1 + 127, 0) - down, 1)
    scale = np.exp2(byte - 127.0)
    codes = (blocks / scale).astype(np.float32).astype(dtype).astype(np.float64)
    return np.moveaxis((codes * scale).reshape(v.shape), -1, axis)


WIDE = False


def mx_kscale(k):
    if not WIDE:
        return np.ones(k)
    levels = np.array([10, -10, 5, -5, 0])
    if k % 512:
        return np.exp2(np.random.permutation(np.resize(levels, k // 32))).repeat(32)
    a = np.empty((k // 512, 16))
    for p in range(k // 512):
        a[p, :8] = np.random.permutation(np.resize(levels, 8))
        for g in range(8):
            far = levels[np.abs(levels - a[p, g]) >= 10]
            a[p, g + 8] = far[np.random.randint(len(far))]
    return np.exp2(a.ravel()).repeat(32)


def f64(x):
    return np.asarray(x).astype(np.float64)


def striped(idx):
    return np.tile(idx.reshape(-1, 16).T, (8, 1)).astype(np.uint16)


def unstriped(offs):
    return offs[:16].T.reshape(-1).astype(np.int64)


E2M1 = np.array([0.0, 0.5, 1.0, 1.5, 2.0, 3.0, 4.0, 6.0, -0.0, -0.5, -1.0, -1.5, -2.0, -3.0, -4.0, -6.0])


def pack_weight(w, fmt):
    k, n = w.shape
    w = f64(np.asarray(w, np.float32).astype(ml_dtypes.bfloat16)).reshape(k // 32, 32, n)
    amax = np.abs(w).max(1)
    if fmt == "e4m3":
        byte = np.frexp(amax)[1] - 1 + 127 - 7
    else:
        mant, ex = np.frexp(amax / 6.0)
        byte = np.where(mant > 0.5, ex, ex - 1) + 127
    byte = np.clip(np.where(amax > 0, byte, 1), 1, 254)
    scaled = (w * np.exp2(127.0 - byte)[:, None, :]).reshape(k, n).astype(np.float32)
    by_word = np.ascontiguousarray(scaled.reshape(k // 512, 128, 4, n).transpose(0, 1, 3, 2))
    if fmt == "e4m3":
        words = by_word.astype(ml_dtypes.float8_e4m3fn).view(np.uint8)
    else:
        c = by_word.astype(ml_dtypes.float4_e2m1fn).view(np.uint8) & 0xF
        words = (c[..., 0::2] | (c[..., 1::2] << 4)).reshape(k // 512, 128, 2 * n)
    return np.ascontiguousarray(words), np.ascontiguousarray(byte.astype(np.uint8).reshape(k // 512, 16, n))


def unpack_weight(words, scales, fmt):
    g, _, n = scales.shape
    words = np.ascontiguousarray(words).reshape(g, 128, n, -1)
    if fmt == "e4m3":
        vals = words.view(ml_dtypes.float8_e4m3fn).astype(np.float64)
    else:
        nib = np.empty((g, 128, n, 4), np.uint8)
        nib[..., 0::2] = words & 0xF
        nib[..., 1::2] = words >> 4
        vals = E2M1[nib]
    vals = vals * np.repeat(np.exp2(scales.astype(np.float64) - 127.0), 8, axis=1)[..., None]
    return vals.transpose(0, 1, 3, 2).reshape(g * 512, n)


K, T, E, C, N = 2560, 768, 12, 128, 128
K8 = 1024


def by_expert(wq, xq):
    return np.concatenate([wq[e].T @ xq[:, e * C:(e + 1) * C] for e in range(E)], axis=1)


def setup_inputs():
    n = np.random.standard_normal
    s = mx_kscale(K)[:, None]
    first = np.random.permutation(np.repeat(np.arange(E), T // E))
    second = (first + 1 + np.random.permutation(np.repeat(np.arange(E - 1), -(-T // (E - 1)))[:T])) % E
    while np.bincount(second, minlength=E).max() != T // E:
        load = np.bincount(second, minlength=E); hi, lo = int(load.argmax()), int(load.argmin())
        t = np.flatnonzero((second == hi) & (first != lo))[0]; second[t] = lo
    slot_token = np.empty(E * C, np.int64); pos = np.empty((2, T), np.int64); fill = np.zeros(E, np.int64)
    place = np.stack([np.random.permutation(C) for _ in range(E)])
    for r, deal in enumerate((first, second)):
        for t in np.random.permutation(T):
            e = deal[t]; j = e * C + place[e, fill[e]]; fill[e] += 1; slot_token[j] = t; pos[r, t] = j
    g = np.random.uniform(0.2, 0.8, T)
    w = n((E, K, N)) / np.sqrt(K) / s[None]
    w8 = [pack_weight(m[:K8], "e4m3") for m in w]
    w4 = [pack_weight(m[K8:], "e2m1") for m in w]
    return {
        "xT": (n((K, T)) * s).astype(np.float32),
        "w8_words": np.stack([m[0] for m in w8]),
        "w8_scales": np.stack([m[1] for m in w8]),
        "w4_words": np.stack([m[0] for m in w4]),
        "w4_scales": np.stack([m[1] for m in w4]),
        "gate": np.stack([np.tile(g, (N, 1)), np.tile(1.0 - g, (N, 1))]).astype(np.float32),
        "offs": striped(slot_token),
        "pos1": striped(pos[0]),
        "pos2": striped(pos[1]),
    }


def reference(xT, w8_words, w8_scales, w4_words, w4_scales, gate, offs, pos1, pos2):
    idx = unstriped(offs)
    w = np.stack([np.concatenate([unpack_weight(w8_words[e], w8_scales[e], "e4m3"), unpack_weight(w4_words[e], w4_scales[e], "e2m1")]) for e in range(E)])
    xq = mxq(f64(xT)[:, idx], 0, "e4m3")
    y = by_expert(w, xq)
    return f64(gate[0]) * y[:, unstriped(pos1)] + f64(gate[1]) * y[:, unstriped(pos2)]

@@ -1,0 +1,216 @@
+from contextlib import ExitStack
+
+import concourse.mybir as mybir
+
+F32 = mybir.dt.float32
+BF16 = mybir.dt.bfloat16
+I32 = mybir.dt.int32
+U32 = mybir.dt.uint32
+U16 = mybir.dt.uint16
+U8 = mybir.dt.uint8
+FP8X4 = mybir.dt.float8_e4m3fn_x4
+FP4X4 = mybir.dt.float4_e2m1fn_x4
+COPY = mybir.ActivationFunctionType.Copy
+MULT = mybir.AluOpType.mult
+ADD = mybir.AluOpType.add
+
+P = 128
+K, T, E, C, N = 2560, 768, 12, 128, 128
+S = E * C
+PASSES = K // 512
+FLOPS = 2 * K * N * S
+
+ORDER = (2, 3, 0, 1, 4)
+ROW = {2: 0, 3: 4, 4: 0, 0: 4, 1: 8}
+WIDE = 2048
+PIECES = ((0, 512), (512, 768))
+LOADS = {2: ((0, 512), (512, 768)), 3: ((0, 256), (256, 512), (512, 768))}
+GROUP = 4 * (2 * 4 * N + 3 * 2 * N)
+
+
+def tile_moe_pln_lin_none_kernel(tc, xT, w8_words, w8_scales, w4_words, w4_scales, gate, offs, pos1, pos2, out):
+    nc = tc.nc
+    with ExitStack() as ctx:
+        keep = ctx.enter_context(tc.tile_pool(name="keep", bufs=1))
+        psum = ctx.enter_context(tc.psum_pool(name="psum", bufs=1))
+
+        offs_t = keep.tile([P, S // 16], U16, name="offs_t")
+        pos1_t = keep.tile([P, T // 16], U16, name="pos1_t")
+        pos2_t = keep.tile([P, T // 16], U16, name="pos2_t")
+        gate_t = keep.tile([P, 2, T], F32, name="gate_t")
+
+        plane_a = keep.tile([P, WIDE], U8, name="plane_a", tag="shared_a", align_bytes=64)
+        plane_b = keep.tile([P, WIDE], U8, name="plane_b", tag="shared", align_bytes=64)
+        w8s = keep.tile([P, E, 2, N], U8, name="w8s", align_bytes=64)
+        w4s = keep.tile([P, E, 3, N], U8, name="w4s", align_bytes=64)
+        moved = keep.tile([P, S], U8, name="moved", align_bytes=64)
+        for t in (plane_b[:], w8s[:].rearrange("p e a n -> p (e a n)"), w4s[:].rearrange("p e a n -> p (e a n)"), plane_a[:], moved[:]):
+            nc.gpsimd.memset(t.bitcast(I32), 0)
+        codes = {}
+        for a in ORDER:
+            wide = a in ORDER[:3]
+            codes[a] = keep.tile([P, WIDE if wide else T], I32, name=f"codes{a}", align_bytes=64)
+            if wide:
+                nc.vector.memset(codes[a][:, T:WIDE], 0)
+
+        x_view = xT.rearrange("(a p j) t -> a p j t", p=P, j=4)
+        raw = {}
+        for i, a in enumerate(ORDER):
+            for lo, hi in LOADS.get(a, ((0, T),)):
+                part = keep.tile([P, 4, hi - lo], F32, name=f"raw{a}_{lo}")
+                nc.sync.dma_start(part[:], x_view[a][:, :, lo:hi])
+                raw.setdefault(a, []).append((lo, hi, part))
+            if i == 0:
+                nc.sync.dma_start(offs_t[:], offs)
+        for scales, source in ((w4s, w4_scales), (w8s, w8_scales)):
+            for q in range(4):
+                nc.sync.dma_start(
+                    scales[32 * q : 32 * q + 4].rearrange("p e a n -> p (e a) n").bitcast(I32),
+                    source[:, :, 4 * q : 4 * q + 4, :].rearrange("e a q n -> q (e a) n").bitcast(I32),
+                )
+        w8_view = w8_words.rearrange("e a p n r -> p (e a) (n r)")
+        w4_view = w4_words.rearrange("e a p b -> p (e a) b")
+
+        def load_words(dst, g):
+            half = 4 * 2 * 4 * N
+            nc.sync.dma_start(dst[:, :half].rearrange("p (x b) -> p x b", b=4 * N).bitcast(I32), w8_view[:, 8 * g : 8 * g + 8, :].bitcast(I32))
+            nc.sync.dma_start(dst[:, half:].rearrange("p (x b) -> p x b", b=2 * N).bitcast(I32), w4_view[:, 12 * g : 12 * g + 12, :].bitcast(I32))
+
+        words_0 = keep.tile([P, GROUP], U8, name="words_0", align_bytes=64)
+        load_words(words_0[:], 0)
+        words = [words_0[:]]
+
+        grouped = [keep.tile([P, T, 4], BF16, name=f"grouped{a}", align_bytes=64) for a in range(PASSES)]
+        slot_words = {a: keep.tile([P, S], U32, name=f"slot_words{a}", align_bytes=64) for a in (2, 3, 0, 4)}
+        bytes_a = keep.tile([P, S], U8, name="bytes_a", align_bytes=64)
+        bytes_b = keep.tile([P, S], U8, name="bytes_b", align_bytes=64)
+        y = keep.tile([P, S], F32, name="y")
+
+        def cast(a, lo, hi, on_vector=False):
+            for base, end, part in raw[a]:
+                if base <= lo and hi <= end:
+                    dst = grouped[a][:, lo:hi, :].rearrange("p (c i) t -> p c t i", i=4)
+                    from_raw = part[:, :, lo - base : hi - base].rearrange("p t (c i) -> p c t i", i=4)
+                    if on_vector:
+                        nc.vector.tensor_copy(dst, from_raw)
+                    else:
+                        nc.scalar.activation(dst, from_raw, COPY)
+
+        def quantise(a, lo, hi):
+            plane = plane_b if a in ORDER[:2] else plane_a
+            nc.vector.quantize_mx(
+                out=codes[a][:, lo:hi].bitcast(FP8X4),
+                scales=plane[ROW[a] : P, lo:hi],
+                in_=grouped[a][:, lo:hi, :].rearrange("p t j -> p (t j)"),
+            )
+
+        def gather_words(a, lo=0, hi=S):
+            nc.vector.tensor_copy(slot_words[a][:, lo:hi], codes[a][:].bitcast(U32).indirect(offs_t[:, lo // 16 : hi // 16]))
+
+        def gather_bytes(dst, plane):
+            nc.vector.tensor_copy(dst[:], plane[:].indirect(offs_t[:]))
+
+        banks = {}
+
+        def multiply(a, experts):
+            for e in experts:
+                if a == ORDER[0]:
+                    banks[e] = psum.tile([N, C], F32, name=f"bank{e % 8}")
+                cols = slice(e * C, (e + 1) * C)
+                if a < 2:
+                    start = ((e % 4) * 2 + a) * 4 * N
+                    lhsT, lscale = words[e // 4][:, start : start + 4 * N].bitcast(FP8X4), w8s[:, e, a, :]
+                else:
+                    start = 4 * 2 * 4 * N + ((e % 4) * 3 + a - 2) * 2 * N
+                    lhsT, lscale = words[e // 4][:, start : start + 2 * N].bitcast(FP4X4), w4s[:, e, a - 2, :]
+                if a == 2:
+                    rscale = bytes_b[:, cols]
+                elif a == 3:
+                    rscale = moved[:, cols]
+                else:
+                    rscale = bytes_a[ROW[a] : P, cols]
+                nc.tensor.matmul_mx(
+                    out=banks[e][:], lhsT=lhsT, lhsT_scale=lscale,
+                    rhs=slot_words[a][:, cols].bitcast(FP8X4), rhs_scale=rscale,
+                    start=(a == ORDER[0]), stop=(a == ORDER[-1]),
+                )
+
+        def empty(e, on_vector=False):
+            dst = y[:, e * C : (e + 1) * C]
+            if on_vector:
+                nc.vector.tensor_copy(dst, banks[e][:])
+            else:
+                nc.scalar.copy(dst, banks[e][:])
+
+        cast(2, 0, 320, on_vector=True)
+        cast(2, 320, 512)
+        quantise(2, 0, 512)
+        cast(2, 512, 640, on_vector=True)
+        cast(2, 640, 768)
+        quantise(2, 512, 768)
+        for lo in (0, 256, 512):
+            cast(3, lo, lo + 256)
+        for a in (0, 1, 4):
+            for lo, hi in PIECES:
+                cast(a, lo, hi)
+        gather_words(2)
+        for lo, hi in PIECES:
+            quantise(3, lo, hi)
+        gather_words(3)
+        gather_bytes(bytes_b, plane_b)
+        for r in range(4):
+            nc.sync.dma_start(moved[r:P:32, :].bitcast(I32), bytes_b[4 + r : P : 32, :].bitcast(I32))
+        later = keep.tile([P, 2 * GROUP], U8, name="later", tag="shared", align_bytes=64)
+        for g in (1, 2):
+            words.append(later[:, (g - 1) * GROUP : g * GROUP])
+            load_words(words[g], g)
+        nc.sync.dma_start(pos1_t[:], pos1)
+        nc.sync.dma_start(pos2_t[:], pos2)
+        nc.sync.dma_start(gate_t[:], gate.rearrange("g p t -> p g t"))
+        A, B, CD = range(0, 4), range(4, 8), range(8, 12)
+        for experts in (A, B):
+            for a in (2, 3):
+                multiply(a, experts)
+        for lo, hi in PIECES:
+            quantise(0, lo, hi)
+        gather_words(0, 0, 1024)
+        for lo, hi in PIECES:
+            quantise(1, lo, hi)
+        gather_words(0, 1024, S)
+        for lo, hi in PIECES:
+            quantise(4, lo, hi)
+        gather_bytes(bytes_a, plane_a)
+        slot_words[1] = keep.tile([P, S], U32, name="slot_words1", tag="shared_a", align_bytes=64)
+        multiply(0, A)
+        multiply(0, B)
+        for lo, experts in ((0, A), (512, B)):
+            gather_words(1, lo, lo + 512)
+            gather_words(4, lo, lo + 512)
+            multiply(1, experts)
+            multiply(4, experts)
+            for e in experts:
+                empty(e)
+        gather_words(1, 1024, S)
+        for a in (2, 3, 0, 1):
+            multiply(a, CD)
+        for lo in (1024, 1280):
+            gather_words(4, lo, lo + 256)
+            e = lo // C
+            multiply(4, (e, e + 1))
+            empty(e)
+            empty(e + 1, on_vector=True)
+
+        part = {}
+
+        def finish(lo, hi):
+            total = keep.tile([P, hi - lo], F32, name=f"total{lo}")
+            nc.vector.tensor_tensor(total[:], part[lo, 0][:], part[lo, 1][:], ADD)
+            nc.sync.dma_start(out[:, lo:hi], total[:])
+
+        for lo, hi in ((0, 384), (384, 768)):
+            for g, pos in enumerate((pos1_t, pos2_t)):
+                part[lo, g] = keep.tile([P, hi - lo], F32, name=f"part{lo}_{g}")
+                nc.vector.tensor_tensor(part[lo, g][:], y[:].indirect(pos[:, lo // 16 : hi // 16]), gate_t[:, g, lo:hi], MULT)
+                if lo and g == 0:
+                    finish(0, 384)
+        finish(384, 768)

@@ -18,14 +18,23 @@ P = 128
 K, T, E, C, N = 2560, 768, 12, 128, 128
 S = E * C
 PASSES = K // 512
+FP8_PASSES = 2
+FP4_PASSES = PASSES - FP8_PASSES
 FLOPS = 2 * K * N * S
 
-ORDER = (2, 3, 0, 1, 4)
-ROW = {2: 0, 3: 4, 4: 0, 0: 4, 1: 8}
-WIDE = 2048
-PIECES = ((0, 512), (512, 768))
-LOADS = {2: ((0, 512), (512, 768)), 3: ((0, 256), (256, 512), (512, 768))}
-GROUP = 4 * (2 * 4 * N + 3 * 2 * N)
+ORDER = (2, 3, 4, 0, 1)
+ROW = {2: 0, 3: 0, 4: 12, 0: 4, 1: 8}
+MOVED_PASS = 4
+MOVED_ROWS = 112
+HALVES = ((0, 512), (512, T))
+WHOLE = ((0, T),)
+LOADS = (HALVES, HALVES, WHOLE, WHOLE, WHOLE)
+GROUP = 4
+GROUPS = E // GROUP
+GROUP_SLOTS = GROUP * C
+W8 = GROUP * FP8_PASSES * 4 * N
+W4 = GROUP * FP4_PASSES * 2 * N
+OUT_PIECES = ((0, 384), (384, 640), (640, T))
 
 
 def tile_moe_pln_lin_none_kernel(tc, xT, w8_words, w8_scales, w4_words, w4_scales, gate, offs, pos1, pos2, out):
@@ -37,102 +46,147 @@ def tile_moe_pln_lin_none_kernel(tc, xT, w8_words, w8_scales, w4_words, w4_scale
         offs_t = keep.tile([P, S // 16], U16, name="offs_t")
         pos1_t = keep.tile([P, T // 16], U16, name="pos1_t")
         pos2_t = keep.tile([P, T // 16], U16, name="pos2_t")
-        gate_t = keep.tile([P, 2, T], F32, name="gate_t")
 
-        plane_a = keep.tile([P, WIDE], U8, name="plane_a", tag="shared_a", align_bytes=64)
-        plane_b = keep.tile([P, WIDE], U8, name="plane_b", tag="shared", align_bytes=64)
-        w8s = keep.tile([P, E, 2, N], U8, name="w8s", align_bytes=64)
-        w4s = keep.tile([P, E, 3, N], U8, name="w4s", align_bytes=64)
-        moved = keep.tile([P, S], U8, name="moved", align_bytes=64)
-        for t in (plane_b[:], w8s[:].rearrange("p e a n -> p (e a n)"), w4s[:].rearrange("p e a n -> p (e a n)"), plane_a[:], moved[:]):
-            nc.gpsimd.memset(t.bitcast(I32), 0)
-        codes = {}
-        for a in ORDER:
-            wide = a in ORDER[:3]
-            codes[a] = keep.tile([P, WIDE if wide else T], I32, name=f"codes{a}", align_bytes=64)
-            if wide:
-                nc.vector.memset(codes[a][:, T:WIDE], 0)
+        first_plane = keep.tile([P, T], U8, name="first_plane", align_bytes=64)
+        planes = keep.tile([P, T], U8, name="planes", tag="planes", align_bytes=64)
+        w4s = keep.tile([P, E * FP4_PASSES, N], U8, name="w4s", align_bytes=64)
+        w8s = keep.tile([P, E * FP8_PASSES, N], U8, name="w8s", align_bytes=64)
+        moved = [keep.tile([P, GROUP_SLOTS], U8, name=f"moved{g}", align_bytes=64) for g in range(GROUPS)]
+        for t in (first_plane[:], planes[:], w4s[:].rearrange("p x n -> p (x n)"), w8s[:].rearrange("p x n -> p (x n)")):
+            nc.vector.memset(t.bitcast(I32), 0)
+        for t in moved:
+            nc.vector.memset(t[96:P, :].bitcast(I32), 0)
 
         x_view = xT.rearrange("(a p j) t -> a p j t", p=P, j=4)
         raw = {}
         for i, a in enumerate(ORDER):
-            for lo, hi in LOADS.get(a, ((0, T),)):
-                part = keep.tile([P, 4, hi - lo], F32, name=f"raw{a}_{lo}")
+            raw[a] = []
+            for lo, hi in LOADS[i]:
+                part = keep.tile([P, 4, hi - lo], F32, name=f"raw{a}_{lo}", tag=f"raw{a}_{hi}", align_bytes=64)
                 nc.sync.dma_start(part[:], x_view[a][:, :, lo:hi])
-                raw.setdefault(a, []).append((lo, hi, part))
+                raw[a].append((lo, hi, part))
             if i == 0:
-                nc.sync.dma_start(offs_t[:], offs)
-        for scales, source in ((w4s, w4_scales), (w8s, w8_scales)):
-            for q in range(4):
-                nc.sync.dma_start(
-                    scales[32 * q : 32 * q + 4].rearrange("p e a n -> p (e a) n").bitcast(I32),
-                    source[:, :, 4 * q : 4 * q + 4, :].rearrange("e a q n -> q (e a) n").bitcast(I32),
-                )
-        w8_view = w8_words.rearrange("e a p n r -> p (e a) (n r)")
-        w4_view = w4_words.rearrange("e a p b -> p (e a) b")
+                for tile, source in ((offs_t, offs), (pos1_t, pos1), (pos2_t, pos2)):
+                    nc.sync.dma_start(tile[:], source)
 
-        def load_words(dst, g):
-            half = 4 * 2 * 4 * N
-            nc.sync.dma_start(dst[:, :half].rearrange("p (x b) -> p x b", b=4 * N).bitcast(I32), w8_view[:, 8 * g : 8 * g + 8, :].bitcast(I32))
-            nc.sync.dma_start(dst[:, half:].rearrange("p (x b) -> p x b", b=2 * N).bitcast(I32), w4_view[:, 12 * g : 12 * g + 12, :].bitcast(I32))
+        views = {
+            FP8_PASSES: w8_words.rearrange("e a p n r -> p (e a) (n r)"),
+            FP4_PASSES: w4_words.rearrange("e a p b -> p (e a) b"),
+        }
+        words = {}
 
-        words_0 = keep.tile([P, GROUP], U8, name="words_0", align_bytes=64)
-        load_words(words_0[:], 0)
-        words = [words_0[:]]
+        def load_words(passes, g, tile):
+            rows = tile[:].rearrange("p (x b) -> p x b", x=GROUP * passes)
+            nc.sync.dma_start(rows.bitcast(I32), views[passes][:, GROUP * passes * g : GROUP * passes * (g + 1), :].bitcast(I32))
+            words[passes, g] = rows
 
-        grouped = [keep.tile([P, T, 4], BF16, name=f"grouped{a}", align_bytes=64) for a in range(PASSES)]
-        slot_words = {a: keep.tile([P, S], U32, name=f"slot_words{a}", align_bytes=64) for a in (2, 3, 0, 4)}
-        bytes_a = keep.tile([P, S], U8, name="bytes_a", align_bytes=64)
-        bytes_b = keep.tile([P, S], U8, name="bytes_b", align_bytes=64)
-        y = keep.tile([P, S], F32, name="y")
+        def load_scales(scales, source):
+            for r in range(4):
+                nc.sync.dma_start(scales[r:P:32].bitcast(I32), source[:, :, r:16:4, :].rearrange("e a q n -> q (e a) n").bitcast(I32))
+
+        for g in range(GROUPS):
+            load_words(FP4_PASSES, g, keep.tile([P, W4], U8, name=f"fp4_words{g}", align_bytes=64))
+            if g == 0:
+                load_scales(w4s, w4_scales)
+            load_words(FP8_PASSES, g, keep.tile([P, W8], U8, name=f"fp8_words{g}", align_bytes=64))
+            if g == 0:
+                load_scales(w8s, w8_scales)
+
+        grouped = {a: keep.tile([P, T, 4], BF16, name=f"grouped{a}", align_bytes=64) for a in ORDER}
+        codes = {a: keep.tile([P, T], U32, name=f"codes{a}", align_bytes=64) for a in ORDER}
 
         def cast(a, lo, hi, on_vector=False):
             for base, end, part in raw[a]:
                 if base <= lo and hi <= end:
                     dst = grouped[a][:, lo:hi, :].rearrange("p (c i) t -> p c t i", i=4)
-                    from_raw = part[:, :, lo - base : hi - base].rearrange("p t (c i) -> p c t i", i=4)
+                    src = part[:, :, lo - base : hi - base].rearrange("p t (c i) -> p c t i", i=4)
                     if on_vector:
-                        nc.vector.tensor_copy(dst, from_raw)
+                        nc.vector.tensor_copy(dst, src)
                     else:
-                        nc.scalar.activation(dst, from_raw, COPY)
+                        nc.scalar.activation(dst, src, COPY)
 
         def quantise(a, lo, hi):
-            plane = plane_b if a in ORDER[:2] else plane_a
+            plane = first_plane if a == ORDER[0] else planes
             nc.vector.quantize_mx(
                 out=codes[a][:, lo:hi].bitcast(FP8X4),
                 scales=plane[ROW[a] : P, lo:hi],
                 in_=grouped[a][:, lo:hi, :].rearrange("p t j -> p (t j)"),
             )
 
-        def gather_words(a, lo=0, hi=S):
-            nc.vector.tensor_copy(slot_words[a][:, lo:hi], codes[a][:].bitcast(U32).indirect(offs_t[:, lo // 16 : hi // 16]))
+        def prepare(a):
+            for lo, hi in HALVES:
+                cast(a, lo, hi)
+            for lo, hi in HALVES:
+                quantise(a, lo, hi)
 
-        def gather_bytes(dst, plane):
-            nc.vector.tensor_copy(dst[:], plane[:].indirect(offs_t[:]))
+        def gather(dst, window, lo, hi):
+            nc.vector.tensor_copy(dst, window[:].indirect(offs_t[:, lo // 16 : hi // 16]))
 
+        slots = {}
+
+        def gather_group(what, window, dtype, g, behind=None):
+            tag = f"{what}_{g}" if behind is None else f"raw{behind}_{T}"
+            slots[what, g] = keep.tile([P, GROUP_SLOTS], dtype, name=f"{what}_{g}", tag=tag, align_bytes=64)[:]
+            gather(slots[what, g], window, g * GROUP_SLOTS, (g + 1) * GROUP_SLOTS)
+
+        first, second, third, fourth, last = ORDER
+        cast(first, 0, 320, on_vector=True)
+        cast(first, 320, 512)
+        quantise(first, 0, 512)
+        cast(first, 512, 640, on_vector=True)
+        cast(first, 640, T)
+        quantise(first, 512, T)
+        for g in range(GROUPS):
+            gather_group(f"words{first}", codes[first], U32, g)
+        for g in (0, 1):
+            gather_group("first_bytes", first_plane, U8, g)
+        prepare(second)
+        gather_group("first_bytes", first_plane, U8, 2, behind=second)
+        for a, following in ((second, third), (third, fourth)):
+            for g in (0, 1):
+                gather_group(f"words{a}", codes[a], U32, g)
+            prepare(following)
+            gather_group(f"words{a}", codes[a], U32, 2, behind=following)
+        prepare(last)
+        held = keep.tile([P, GROUPS, GROUP_SLOTS], U32, name="held", tag=f"raw{last}_{T}", align_bytes=64)
+
+        def gather_fourth(g):
+            slots[f"words{fourth}", g] = held[:, g, :]
+            gather(held[:, g, :], codes[fourth], g * GROUP_SLOTS, (g + 1) * GROUP_SLOTS)
+
+        gather_fourth(0)
+        for g in range(GROUPS):
+            gather_group("bytes", planes, U8, g)
+            rows = slice(ROW[MOVED_PASS], ROW[MOVED_PASS] + MOVED_ROWS)
+            nc.sync.dma_start(moved[g][:MOVED_ROWS, :].bitcast(I32), slots["bytes", g][rows, :].bitcast(I32))
+        gate_t = keep.tile([P, 2, T], F32, name="gate_t", tag="planes", align_bytes=64)
+        nc.sync.dma_start(gate_t[:], gate.rearrange("g p t -> p g t"))
+
+        y = keep.tile([P, S], F32, name="y")
         banks = {}
 
-        def multiply(a, experts):
+        def multiply(a, experts, start=False, stop=False):
             for e in experts:
-                if a == ORDER[0]:
-                    banks[e] = psum.tile([N, C], F32, name=f"bank{e % 8}")
-                cols = slice(e * C, (e + 1) * C)
-                if a < 2:
-                    start = ((e % 4) * 2 + a) * 4 * N
-                    lhsT, lscale = words[e // 4][:, start : start + 4 * N].bitcast(FP8X4), w8s[:, e, a, :]
+                g, m = divmod(e, GROUP)
+                if start:
+                    banks[e] = psum.tile([N, C], F32, name=f"sum{e}", tag=f"bank{e % 8}")
+                cols = slice(m * C, (m + 1) * C)
+                if a < FP8_PASSES:
+                    lhsT = words[FP8_PASSES, g][:, m * FP8_PASSES + a, :].bitcast(FP8X4)
+                    lhsT_scale = w8s[:, e * FP8_PASSES + a, :]
                 else:
-                    start = 4 * 2 * 4 * N + ((e % 4) * 3 + a - 2) * 2 * N
-                    lhsT, lscale = words[e // 4][:, start : start + 2 * N].bitcast(FP4X4), w4s[:, e, a - 2, :]
-                if a == 2:
-                    rscale = bytes_b[:, cols]
-                elif a == 3:
-                    rscale = moved[:, cols]
+                    lhsT = words[FP4_PASSES, g][:, m * FP4_PASSES + a - FP8_PASSES, :].bitcast(FP4X4)
+                    lhsT_scale = w4s[:, e * FP4_PASSES + a - FP8_PASSES, :]
+                if a == first:
+                    rhs_scale = slots["first_bytes", g][:, cols]
+                elif a == MOVED_PASS:
+                    rhs_scale = moved[g][:, cols]
                 else:
-                    rscale = bytes_a[ROW[a] : P, cols]
+                    rhs_scale = slots["bytes", g][ROW[a] : P, cols]
                 nc.tensor.matmul_mx(
-                    out=banks[e][:], lhsT=lhsT, lhsT_scale=lscale,
-                    rhs=slot_words[a][:, cols].bitcast(FP8X4), rhs_scale=rscale,
-                    start=(a == ORDER[0]), stop=(a == ORDER[-1]),
+                    out=banks[e][:], lhsT=lhsT, lhsT_scale=lhsT_scale,
+                    rhs=slots[f"words{a}", g][:, cols].bitcast(FP8X4), rhs_scale=rhs_scale,
+                    start=start, stop=stop,
                 )
 
         def empty(e, on_vector=False):
@@ -142,63 +196,35 @@ def tile_moe_pln_lin_none_kernel(tc, xT, w8_words, w8_scales, w4_words, w4_scale
             else:
                 nc.scalar.copy(dst, banks[e][:])
 
-        cast(2, 0, 320, on_vector=True)
-        cast(2, 320, 512)
-        quantise(2, 0, 512)
-        cast(2, 512, 640, on_vector=True)
-        cast(2, 640, 768)
-        quantise(2, 512, 768)
-        for lo in (0, 256, 512):
-            cast(3, lo, lo + 256)
-        for a in (0, 1, 4):
-            for lo, hi in PIECES:
-                cast(a, lo, hi)
-        gather_words(2)
-        for lo, hi in PIECES:
-            quantise(3, lo, hi)
-        gather_words(3)
-        gather_bytes(bytes_b, plane_b)
-        for r in range(4):
-            nc.sync.dma_start(moved[r:P:32, :].bitcast(I32), bytes_b[4 + r : P : 32, :].bitcast(I32))
-        later = keep.tile([P, 2 * GROUP], U8, name="later", tag="shared", align_bytes=64)
-        for g in (1, 2):
-            words.append(later[:, (g - 1) * GROUP : g * GROUP])
-            load_words(words[g], g)
-        nc.sync.dma_start(pos1_t[:], pos1)
-        nc.sync.dma_start(pos2_t[:], pos2)
-        nc.sync.dma_start(gate_t[:], gate.rearrange("g p t -> p g t"))
-        A, B, CD = range(0, 4), range(4, 8), range(8, 12)
-        for experts in (A, B):
-            for a in (2, 3):
-                multiply(a, experts)
-        for lo, hi in PIECES:
-            quantise(0, lo, hi)
-        gather_words(0, 0, 1024)
-        for lo, hi in PIECES:
-            quantise(1, lo, hi)
-        gather_words(0, 1024, S)
-        for lo, hi in PIECES:
-            quantise(4, lo, hi)
-        gather_bytes(bytes_a, plane_a)
-        slot_words[1] = keep.tile([P, S], U32, name="slot_words1", tag="shared_a", align_bytes=64)
-        multiply(0, A)
-        multiply(0, B)
-        for lo, experts in ((0, A), (512, B)):
-            gather_words(1, lo, lo + 512)
-            gather_words(4, lo, lo + 512)
-            multiply(1, experts)
-            multiply(4, experts)
-            for e in experts:
-                empty(e)
-        gather_words(1, 1024, S)
-        for a in (2, 3, 0, 1):
-            multiply(a, CD)
-        for lo in (1024, 1280):
-            gather_words(4, lo, lo + 256)
-            e = lo // C
-            multiply(4, (e, e + 1))
+        group_a, group_b, group_c = (range(g * GROUP, (g + 1) * GROUP) for g in range(GROUPS))
+        for experts in (group_a, group_b):
+            multiply(first, experts, start=True)
+        multiply(second, group_a)
+        multiply(fourth, group_a)
+        multiply(second, group_b)
+        gather_group(f"words{last}", codes[last], U32, 0)
+        multiply(last, group_a)
+        multiply(third, group_a, stop=True)
+        for e in group_a:
             empty(e)
-            empty(e + 1, on_vector=True)
+        gather_fourth(1)
+        gather_group(f"words{last}", codes[last], U32, 1)
+        multiply(fourth, group_b)
+        multiply(third, group_b)
+        multiply(first, group_c, start=True)
+        multiply(second, group_c)
+        multiply(last, group_b, stop=True)
+        for e in group_b:
+            empty(e)
+        gather_fourth(2)
+        multiply(third, group_c)
+        multiply(fourth, group_c)
+        slots[f"words{last}", 2] = keep.tile([P, GROUP_SLOTS], U32, name="last_slots", align_bytes=64)[:]
+        for lo, hi in ((8, 10), (10, 11), (11, 12)):
+            gather(slots[f"words{last}", 2][:, (lo - 8) * C : (hi - 8) * C], codes[last], lo * C, hi * C)
+            multiply(last, range(lo, hi), stop=True)
+            for e in range(lo, hi):
+                empty(e, on_vector=(e == E - 1))
 
         part = {}
 
@@ -207,10 +233,10 @@ def tile_moe_pln_lin_none_kernel(tc, xT, w8_words, w8_scales, w4_words, w4_scale
             nc.vector.tensor_tensor(total[:], part[lo, 0][:], part[lo, 1][:], ADD)
             nc.sync.dma_start(out[:, lo:hi], total[:])
 
-        for lo, hi in ((0, 384), (384, 768)):
+        for i, (lo, hi) in enumerate(OUT_PIECES):
             for g, pos in enumerate((pos1_t, pos2_t)):
                 part[lo, g] = keep.tile([P, hi - lo], F32, name=f"part{lo}_{g}")
                 nc.vector.tensor_tensor(part[lo, g][:], y[:].indirect(pos[:, lo // 16 : hi // 16]), gate_t[:, g, lo:hi], MULT)
-                if lo and g == 0:
-                    finish(0, 384)
-        finish(384, 768)
+                if i and g == 0:
+                    finish(*OUT_PIECES[i - 1])
+        finish(*OUT_PIECES[-1])

@@ -26,7 +26,9 @@ ORDER = (2, 3, 4, 0, 1)
 ROW = {2: 0, 3: 0, 4: 12, 0: 4, 1: 8}
 MOVED_PASS = 4
 MOVED_ROWS = 112
-HALVES = ((0, 512), (512, T))
+HALF = 512
+HALVES = ((0, HALF), (HALF, T))
+LAST_CAST = 16
 WHOLE = ((0, T),)
 LOADS = (HALVES, HALVES, WHOLE, WHOLE, WHOLE)
 GROUP = 4
@@ -62,7 +64,7 @@ def tile_moe_pln_lin_none_kernel(tc, xT, w8_words, w8_scales, w4_words, w4_scale
         for i, a in enumerate(ORDER):
             raw[a] = []
             for lo, hi in LOADS[i]:
-                part = keep.tile([P, 4, hi - lo], F32, name=f"raw{a}_{lo}", tag=f"raw{a}_{hi}", align_bytes=64)
+                part = keep.tile([P, 4, hi - lo], F32, name=f"raw{a}_{lo}", align_bytes=64)
                 nc.sync.dma_start(part[:], x_view[a][:, :, lo:hi])
                 raw[a].append((lo, hi, part))
             if i == 0:
@@ -88,17 +90,23 @@ def tile_moe_pln_lin_none_kernel(tc, xT, w8_words, w8_scales, w4_words, w4_scale
             load_words(FP4_PASSES, g, keep.tile([P, W4], U8, name=f"fp4_words{g}", align_bytes=64))
             if g == 0:
                 load_scales(w4s, w4_scales)
-            load_words(FP8_PASSES, g, keep.tile([P, W8], U8, name=f"fp8_words{g}", align_bytes=64))
+            if g < GROUPS - 1:
+                load_words(FP8_PASSES, g, keep.tile([P, W8], U8, name=f"fp8_words{g}", align_bytes=64))
             if g == 0:
                 load_scales(w8s, w8_scales)
 
-        grouped = {a: keep.tile([P, T, 4], BF16, name=f"grouped{a}", align_bytes=64) for a in ORDER}
+        grouped = {
+            (a, lo): keep.tile([P, hi - lo, 4], BF16, name=f"grouped{a}_{lo}", tag=f"grouped{a}_{lo}", align_bytes=64)
+            for a in ORDER
+            for lo, hi in HALVES
+        }
         codes = {a: keep.tile([P, T], U32, name=f"codes{a}", align_bytes=64) for a in ORDER}
 
         def cast(a, lo, hi, on_vector=False):
             for base, end, part in raw[a]:
                 if base <= lo and hi <= end:
-                    dst = grouped[a][:, lo:hi, :].rearrange("p (c i) t -> p c t i", i=4)
+                    first_token = 0 if hi <= HALF else HALF
+                    dst = grouped[a, first_token][:, lo - first_token : hi - first_token, :].rearrange("p (c i) t -> p c t i", i=4)
                     src = part[:, :, lo - base : hi - base].rearrange("p t (c i) -> p c t i", i=4)
                     if on_vector:
                         nc.vector.tensor_copy(dst, src)
@@ -110,13 +118,13 @@ def tile_moe_pln_lin_none_kernel(tc, xT, w8_words, w8_scales, w4_words, w4_scale
             nc.vector.quantize_mx(
                 out=codes[a][:, lo:hi].bitcast(FP8X4),
                 scales=plane[ROW[a] : P, lo:hi],
-                in_=grouped[a][:, lo:hi, :].rearrange("p t j -> p (t j)"),
+                in_=grouped[a, lo][:].rearrange("p t j -> p (t j)"),
             )
 
         def prepare(a):
-            for lo, hi in HALVES:
+            for lo, hi in ((0, HALF - LAST_CAST), (HALF, T), (HALF - LAST_CAST, HALF)):
                 cast(a, lo, hi)
-            for lo, hi in HALVES:
+            for lo, hi in reversed(HALVES):
                 quantise(a, lo, hi)
 
         def gather(dst, window, lo, hi):
@@ -125,7 +133,7 @@ def tile_moe_pln_lin_none_kernel(tc, xT, w8_words, w8_scales, w4_words, w4_scale
         slots = {}
 
         def gather_group(what, window, dtype, g, behind=None):
-            tag = f"{what}_{g}" if behind is None else f"raw{behind}_{T}"
+            tag = f"{what}_{g}" if behind is None else f"grouped{behind}_{HALF}"
             slots[what, g] = keep.tile([P, GROUP_SLOTS], dtype, name=f"{what}_{g}", tag=tag, align_bytes=64)[:]
             gather(slots[what, g], window, g * GROUP_SLOTS, (g + 1) * GROUP_SLOTS)
 
@@ -148,19 +156,18 @@ def tile_moe_pln_lin_none_kernel(tc, xT, w8_words, w8_scales, w4_words, w4_scale
             prepare(following)
             gather_group(f"words{a}", codes[a], U32, 2, behind=following)
         prepare(last)
-        held = keep.tile([P, GROUPS, GROUP_SLOTS], U32, name="held", tag=f"raw{last}_{T}", align_bytes=64)
+        held = keep.tile([P, GROUPS, GROUP_SLOTS], U32, name="held", tag=f"grouped{last}_{HALF}", align_bytes=64)
 
         def gather_fourth(g):
             slots[f"words{fourth}", g] = held[:, g, :]
             gather(held[:, g, :], codes[fourth], g * GROUP_SLOTS, (g + 1) * GROUP_SLOTS)
 
         gather_fourth(0)
-        for g in range(GROUPS):
+
+        def gather_bytes(g):
             gather_group("bytes", planes, U8, g)
             rows = slice(ROW[MOVED_PASS], ROW[MOVED_PASS] + MOVED_ROWS)
             nc.sync.dma_start(moved[g][:MOVED_ROWS, :].bitcast(I32), slots["bytes", g][rows, :].bitcast(I32))
-        gate_t = keep.tile([P, 2, T], F32, name="gate_t", tag="planes", align_bytes=64)
-        nc.sync.dma_start(gate_t[:], gate.rearrange("g p t -> p g t"))
 
         y = keep.tile([P, S], F32, name="y")
         banks = {}
@@ -199,7 +206,13 @@ def tile_moe_pln_lin_none_kernel(tc, xT, w8_words, w8_scales, w4_words, w4_scale
         group_a, group_b, group_c = (range(g * GROUP, (g + 1) * GROUP) for g in range(GROUPS))
         for experts in (group_a, group_b):
             multiply(first, experts, start=True)
+        gather_bytes(0)
         multiply(second, group_a)
+        load_words(FP8_PASSES, GROUPS - 1, keep.tile([P, W8], U8, name="last_words", tag=f"words{second}_0", align_bytes=64))
+        gather_bytes(1)
+        gather_bytes(2)
+        gate_t = keep.tile([P, 2, T], F32, name="gate_t", tag="planes", align_bytes=64)
+        nc.sync.dma_start(gate_t[:], gate.rearrange("g p t -> p g t"))
         multiply(fourth, group_a)
         multiply(second, group_b)
         gather_group(f"words{last}", codes[last], U32, 0)
@@ -209,10 +222,10 @@ def tile_moe_pln_lin_none_kernel(tc, xT, w8_words, w8_scales, w4_words, w4_scale
             empty(e)
         gather_fourth(1)
         gather_group(f"words{last}", codes[last], U32, 1)
-        multiply(fourth, group_b)
         multiply(third, group_b)
         multiply(first, group_c, start=True)
         multiply(second, group_c)
+        multiply(fourth, group_b)
         multiply(last, group_b, stop=True)
         for e in group_b:
             empty(e)

@@ -21,26 +21,31 @@ PASSES = K // 512
 FP8_PASSES = 2
 FP4_PASSES = PASSES - FP8_PASSES
 FLOPS = 2 * K * N * S
+BANKS = 8
 
 ORDER = (2, 3, 4, 0, 1)
 ROW = {2: 0, 3: 0, 4: 12, 0: 4, 1: 8}
 MOVED_PASS = 4
 MOVED_ROWS = 112
+LAST_QUADRANT = 96
+
 HALF = 512
 HALVES = ((0, HALF), (HALF, T))
-LAST_CAST = 16
 WHOLE = ((0, T),)
 LOADS = (HALVES, HALVES, WHOLE, WHOLE, WHOLE)
+VECTOR_CASTS_TO = (320, 640)
+LAST_CAST = 16
+
 GROUP = 4
 GROUPS = E // GROUP
 GROUP_SLOTS = GROUP * C
-W8 = GROUP * FP8_PASSES * 4 * N
-W4 = GROUP * FP4_PASSES * 2 * N
+LAST_RUNS = ((8, 10), (10, 11), (11, 12))
 OUT_PIECES = ((0, 384), (384, 640), (640, T))
 
 
 def tile_moe_pln_lin_none_kernel(tc, xT, w8_words, w8_scales, w4_words, w4_scales, gate, offs, pos1, pos2, out):
     nc = tc.nc
+    first, second, third, fourth, last = ORDER
     with ExitStack() as ctx:
         keep = ctx.enter_context(tc.tile_pool(name="keep", bufs=1))
         psum = ctx.enter_context(tc.psum_pool(name="psum", bufs=1))
@@ -57,41 +62,43 @@ def tile_moe_pln_lin_none_kernel(tc, xT, w8_words, w8_scales, w4_words, w4_scale
         for t in (first_plane[:], planes[:], w4s[:].rearrange("p x n -> p (x n)"), w8s[:].rearrange("p x n -> p (x n)")):
             nc.vector.memset(t.bitcast(I32), 0)
         for t in moved:
-            nc.vector.memset(t[96:P, :].bitcast(I32), 0)
+            nc.vector.memset(t[LAST_QUADRANT:P, :].bitcast(I32), 0)
 
         x_view = xT.rearrange("(a p j) t -> a p j t", p=P, j=4)
         raw = {}
-        for i, a in enumerate(ORDER):
+        for a, pieces in zip(ORDER, LOADS):
             raw[a] = []
-            for lo, hi in LOADS[i]:
+            for lo, hi in pieces:
                 part = keep.tile([P, 4, hi - lo], F32, name=f"raw{a}_{lo}", align_bytes=64)
                 nc.sync.dma_start(part[:], x_view[a][:, :, lo:hi])
                 raw[a].append((lo, hi, part))
-            if i == 0:
+            if a == first:
                 for tile, source in ((offs_t, offs), (pos1_t, pos1), (pos2_t, pos2)):
                     nc.sync.dma_start(tile[:], source)
 
-        views = {
+        w_views = {
             FP8_PASSES: w8_words.rearrange("e a p n r -> p (e a) (n r)"),
             FP4_PASSES: w4_words.rearrange("e a p b -> p (e a) b"),
         }
-        words = {}
+        w_bytes = {FP8_PASSES: GROUP * FP8_PASSES * 4 * N, FP4_PASSES: GROUP * FP4_PASSES * 2 * N}
+        weights = {}
 
-        def load_words(passes, g, tile):
+        def load_weights(passes, g, tag):
+            tile = keep.tile([P, w_bytes[passes]], U8, name=f"weights{passes}_{g}", tag=tag, align_bytes=64)
             rows = tile[:].rearrange("p (x b) -> p x b", x=GROUP * passes)
-            nc.sync.dma_start(rows.bitcast(I32), views[passes][:, GROUP * passes * g : GROUP * passes * (g + 1), :].bitcast(I32))
-            words[passes, g] = rows
+            nc.sync.dma_start(rows.bitcast(I32), w_views[passes][:, GROUP * passes * g : GROUP * passes * (g + 1), :].bitcast(I32))
+            weights[passes, g] = rows
 
         def load_scales(scales, source):
             for r in range(4):
                 nc.sync.dma_start(scales[r:P:32].bitcast(I32), source[:, :, r:16:4, :].rearrange("e a q n -> q (e a) n").bitcast(I32))
 
         for g in range(GROUPS):
-            load_words(FP4_PASSES, g, keep.tile([P, W4], U8, name=f"fp4_words{g}", align_bytes=64))
+            load_weights(FP4_PASSES, g, f"fp4_{g}")
             if g == 0:
                 load_scales(w4s, w4_scales)
             if g < GROUPS - 1:
-                load_words(FP8_PASSES, g, keep.tile([P, W8], U8, name=f"fp8_words{g}", align_bytes=64))
+                load_weights(FP8_PASSES, g, f"fp8_{g}")
             if g == 0:
                 load_scales(w8s, w8_scales)
 
@@ -103,18 +110,18 @@ def tile_moe_pln_lin_none_kernel(tc, xT, w8_words, w8_scales, w4_words, w4_scale
         codes = {a: keep.tile([P, T], U32, name=f"codes{a}", align_bytes=64) for a in ORDER}
 
         def cast(a, lo, hi, on_vector=False):
+            piece = 0 if hi <= HALF else HALF
+            dst = grouped[a, piece][:, lo - piece : hi - piece, :].rearrange("p (c i) j -> p c j i", i=4)
             for base, end, part in raw[a]:
                 if base <= lo and hi <= end:
-                    first_token = 0 if hi <= HALF else HALF
-                    dst = grouped[a, first_token][:, lo - first_token : hi - first_token, :].rearrange("p (c i) t -> p c t i", i=4)
-                    src = part[:, :, lo - base : hi - base].rearrange("p t (c i) -> p c t i", i=4)
+                    src = part[:, :, lo - base : hi - base].rearrange("p j (c i) -> p c j i", i=4)
                     if on_vector:
                         nc.vector.tensor_copy(dst, src)
                     else:
                         nc.scalar.activation(dst, src, COPY)
 
         def quantise(a, lo, hi):
-            plane = first_plane if a == ORDER[0] else planes
+            plane = first_plane if a == first else planes
             nc.vector.quantize_mx(
                 out=codes[a][:, lo:hi].bitcast(FP8X4),
                 scales=plane[ROW[a] : P, lo:hi],
@@ -137,32 +144,28 @@ def tile_moe_pln_lin_none_kernel(tc, xT, w8_words, w8_scales, w4_words, w4_scale
             slots[what, g] = keep.tile([P, GROUP_SLOTS], dtype, name=f"{what}_{g}", tag=tag, align_bytes=64)[:]
             gather(slots[what, g], window, g * GROUP_SLOTS, (g + 1) * GROUP_SLOTS)
 
-        first, second, third, fourth, last = ORDER
-        cast(first, 0, 320, on_vector=True)
-        cast(first, 320, 512)
-        quantise(first, 0, 512)
-        cast(first, 512, 640, on_vector=True)
-        cast(first, 640, T)
-        quantise(first, 512, T)
+        for (lo, hi), mark in zip(HALVES, VECTOR_CASTS_TO):
+            cast(first, lo, mark, on_vector=True)
+            cast(first, mark, hi)
+            quantise(first, lo, hi)
         for g in range(GROUPS):
             gather_group(f"words{first}", codes[first], U32, g)
-        for g in (0, 1):
+        for g in range(GROUPS - 1):
             gather_group("first_bytes", first_plane, U8, g)
         prepare(second)
-        gather_group("first_bytes", first_plane, U8, 2, behind=second)
+        gather_group("first_bytes", first_plane, U8, GROUPS - 1, behind=second)
         for a, following in ((second, third), (third, fourth)):
-            for g in (0, 1):
+            for g in range(GROUPS - 1):
                 gather_group(f"words{a}", codes[a], U32, g)
             prepare(following)
-            gather_group(f"words{a}", codes[a], U32, 2, behind=following)
+            gather_group(f"words{a}", codes[a], U32, GROUPS - 1, behind=following)
         prepare(last)
-        held = keep.tile([P, GROUPS, GROUP_SLOTS], U32, name="held", tag=f"grouped{last}_{HALF}", align_bytes=64)
+        gather_group(f"words{fourth}", codes[fourth], U32, 0, behind=last)
+        late_fourth = keep.tile([P, GROUPS - 1, GROUP_SLOTS], U32, name="late_fourth", tag=f"grouped{last}_0", align_bytes=64)
 
-        def gather_fourth(g):
-            slots[f"words{fourth}", g] = held[:, g, :]
-            gather(held[:, g, :], codes[fourth], g * GROUP_SLOTS, (g + 1) * GROUP_SLOTS)
-
-        gather_fourth(0)
+        def gather_late_fourth(g):
+            slots[f"words{fourth}", g] = late_fourth[:, g - 1, :]
+            gather(late_fourth[:, g - 1, :], codes[fourth], g * GROUP_SLOTS, (g + 1) * GROUP_SLOTS)
 
         def gather_bytes(g):
             gather_group("bytes", planes, U8, g)
@@ -170,19 +173,19 @@ def tile_moe_pln_lin_none_kernel(tc, xT, w8_words, w8_scales, w4_words, w4_scale
             nc.sync.dma_start(moved[g][:MOVED_ROWS, :].bitcast(I32), slots["bytes", g][rows, :].bitcast(I32))
 
         y = keep.tile([P, S], F32, name="y")
-        banks = {}
+        sums = {}
 
         def multiply(a, experts, start=False, stop=False):
             for e in experts:
                 g, m = divmod(e, GROUP)
                 if start:
-                    banks[e] = psum.tile([N, C], F32, name=f"sum{e}", tag=f"bank{e % 8}")
+                    sums[e] = psum.tile([N, C], F32, name=f"sum{e}", tag=f"bank{e % BANKS}")
                 cols = slice(m * C, (m + 1) * C)
                 if a < FP8_PASSES:
-                    lhsT = words[FP8_PASSES, g][:, m * FP8_PASSES + a, :].bitcast(FP8X4)
+                    lhsT = weights[FP8_PASSES, g][:, m * FP8_PASSES + a, :].bitcast(FP8X4)
                     lhsT_scale = w8s[:, e * FP8_PASSES + a, :]
                 else:
-                    lhsT = words[FP4_PASSES, g][:, m * FP4_PASSES + a - FP8_PASSES, :].bitcast(FP4X4)
+                    lhsT = weights[FP4_PASSES, g][:, m * FP4_PASSES + a - FP8_PASSES, :].bitcast(FP4X4)
                     lhsT_scale = w4s[:, e * FP4_PASSES + a - FP8_PASSES, :]
                 if a == first:
                     rhs_scale = slots["first_bytes", g][:, cols]
@@ -191,7 +194,7 @@ def tile_moe_pln_lin_none_kernel(tc, xT, w8_words, w8_scales, w4_words, w4_scale
                 else:
                     rhs_scale = slots["bytes", g][ROW[a] : P, cols]
                 nc.tensor.matmul_mx(
-                    out=banks[e][:], lhsT=lhsT, lhsT_scale=lhsT_scale,
+                    out=sums[e][:], lhsT=lhsT, lhsT_scale=lhsT_scale,
                     rhs=slots[f"words{a}", g][:, cols].bitcast(FP8X4), rhs_scale=rhs_scale,
                     start=start, stop=stop,
                 )
@@ -199,28 +202,28 @@ def tile_moe_pln_lin_none_kernel(tc, xT, w8_words, w8_scales, w4_words, w4_scale
         def empty(e, on_vector=False):
             dst = y[:, e * C : (e + 1) * C]
             if on_vector:
-                nc.vector.tensor_copy(dst, banks[e][:])
+                nc.vector.tensor_copy(dst, sums[e][:])
             else:
-                nc.scalar.copy(dst, banks[e][:])
+                nc.scalar.copy(dst, sums[e][:])
 
         group_a, group_b, group_c = (range(g * GROUP, (g + 1) * GROUP) for g in range(GROUPS))
         for experts in (group_a, group_b):
             multiply(first, experts, start=True)
         gather_bytes(0)
         multiply(second, group_a)
-        load_words(FP8_PASSES, GROUPS - 1, keep.tile([P, W8], U8, name="last_words", tag=f"words{second}_0", align_bytes=64))
+        load_weights(FP8_PASSES, GROUPS - 1, f"words{second}_0")
         gather_bytes(1)
+        gather_group(f"words{last}", codes[last], U32, 0)
         gather_bytes(2)
         gate_t = keep.tile([P, 2, T], F32, name="gate_t", tag="planes", align_bytes=64)
         nc.sync.dma_start(gate_t[:], gate.rearrange("g p t -> p g t"))
         multiply(fourth, group_a)
         multiply(second, group_b)
-        gather_group(f"words{last}", codes[last], U32, 0)
         multiply(last, group_a)
         multiply(third, group_a, stop=True)
         for e in group_a:
             empty(e)
-        gather_fourth(1)
+        gather_late_fourth(1)
         gather_group(f"words{last}", codes[last], U32, 1)
         multiply(third, group_b)
         multiply(first, group_c, start=True)
@@ -229,27 +232,28 @@ def tile_moe_pln_lin_none_kernel(tc, xT, w8_words, w8_scales, w4_words, w4_scale
         multiply(last, group_b, stop=True)
         for e in group_b:
             empty(e)
-        gather_fourth(2)
+        gather_late_fourth(2)
         multiply(third, group_c)
         multiply(fourth, group_c)
-        slots[f"words{last}", 2] = keep.tile([P, GROUP_SLOTS], U32, name="last_slots", align_bytes=64)[:]
-        for lo, hi in ((8, 10), (10, 11), (11, 12)):
-            gather(slots[f"words{last}", 2][:, (lo - 8) * C : (hi - 8) * C], codes[last], lo * C, hi * C)
+        last_slots = keep.tile([P, GROUP_SLOTS], U32, name="last_slots", align_bytes=64)
+        slots[f"words{last}", GROUPS - 1] = last_slots[:]
+        for lo, hi in LAST_RUNS:
+            gather(last_slots[:, (lo - group_c.start) * C : (hi - group_c.start) * C], codes[last], lo * C, hi * C)
             multiply(last, range(lo, hi), stop=True)
             for e in range(lo, hi):
-                empty(e, on_vector=(e == E - 1))
+                empty(e, on_vector=(e == E - 2))
 
-        part = {}
+        products = {}
 
         def finish(lo, hi):
             total = keep.tile([P, hi - lo], F32, name=f"total{lo}")
-            nc.vector.tensor_tensor(total[:], part[lo, 0][:], part[lo, 1][:], ADD)
+            nc.vector.tensor_tensor(total[:], products[lo, 0][:], products[lo, 1][:], ADD)
             nc.sync.dma_start(out[:, lo:hi], total[:])
 
         for i, (lo, hi) in enumerate(OUT_PIECES):
-            for g, pos in enumerate((pos1_t, pos2_t)):
-                part[lo, g] = keep.tile([P, hi - lo], F32, name=f"part{lo}_{g}")
-                nc.vector.tensor_tensor(part[lo, g][:], y[:].indirect(pos[:, lo // 16 : hi // 16]), gate_t[:, g, lo:hi], MULT)
-                if i and g == 0:
+            for choice, pos in enumerate((pos1_t, pos2_t)):
+                products[lo, choice] = keep.tile([P, hi - lo], F32, name=f"product{lo}_{choice}")
+                nc.vector.tensor_tensor(products[lo, choice][:], y[:].indirect(pos[:, lo // 16 : hi // 16]), gate_t[:, choice, lo:hi], MULT)
+                if i and choice == 0:
                     finish(*OUT_PIECES[i - 1])
         finish(*OUT_PIECES[-1])

@@ -40,7 +40,7 @@ GROUP = 4
 GROUPS = E // GROUP
 GROUP_SLOTS = GROUP * C
 LAST_RUNS = ((8, 10), (10, 11), (11, 12))
-OUT_PIECES = ((0, 384), (384, 640), (640, T))
+OUT_PIECES = ((0, 256, True), (256, 448, False), (448, 640, True), (640, T, True))
 
 
 def tile_moe_pln_lin_none_kernel(tc, xT, w8_words, w8_scales, w4_words, w4_scales, gate, offs, pos1, pos2, out):
@@ -243,17 +243,35 @@ def tile_moe_pln_lin_none_kernel(tc, xT, w8_words, w8_scales, w4_words, w4_scale
             for e in range(lo, hi):
                 empty(e, on_vector=(e == E - 2))
 
-        products = {}
+        pos_t = (pos1_t, pos2_t)
+        fetched, products = {}, {}
+        for lo, hi, fused in OUT_PIECES:
+            fetched[lo] = keep.tile([P, 1 if fused else 2, hi - lo], F32, name=f"fetched{lo}")
+            products[lo] = keep.tile([P, 2, hi - lo], F32, name=f"products{lo}")
+            for j, choice in enumerate((1,) if fused else (0, 1)):
+                nc.scalar.activation(fetched[lo][:, j, :], y[:].indirect(pos_t[choice][:, lo // 16 : hi // 16]), COPY)
 
-        def finish(lo, hi):
+        def fetch_first(lo, hi, fused):
+            nc.vector.tensor_tensor(products[lo][:, 0, :], y[:].indirect(pos1_t[:, lo // 16 : hi // 16]), gate_t[:, 0, lo:hi], MULT)
+
+        def weigh(lo, hi, fused):
+            choices = slice(1, 2) if fused else slice(0, 2)
+            nc.vector.tensor_tensor(products[lo][:, choices, :], fetched[lo][:], gate_t[:, choices, lo:hi], MULT)
+
+        def finish(lo, hi, fused):
             total = keep.tile([P, hi - lo], F32, name=f"total{lo}")
-            nc.vector.tensor_tensor(total[:], products[lo, 0][:], products[lo, 1][:], ADD)
+            nc.vector.tensor_tensor(total[:], products[lo][:, 0, :], products[lo][:, 1, :], ADD)
             nc.sync.dma_start(out[:, lo:hi], total[:])
 
-        for i, (lo, hi) in enumerate(OUT_PIECES):
-            for choice, pos in enumerate((pos1_t, pos2_t)):
-                products[lo, choice] = keep.tile([P, hi - lo], F32, name=f"product{lo}_{choice}")
-                nc.vector.tensor_tensor(products[lo, choice][:], y[:].indirect(pos[:, lo // 16 : hi // 16]), gate_t[:, choice, lo:hi], MULT)
-                if i and choice == 0:
-                    finish(*OUT_PIECES[i - 1])
-        finish(*OUT_PIECES[-1])
+        piece_a, piece_b, piece_c, piece_d = OUT_PIECES
+        fetch_first(*piece_a)
+        fetch_first(*piece_c)
+        weigh(*piece_a)
+        fetch_first(*piece_d)
+        finish(*piece_a)
+        weigh(*piece_b)
+        weigh(*piece_c)
+        finish(*piece_b)
+        weigh(*piece_d)
+        finish(*piece_c)
+        finish(*piece_d)

@@ -26,7 +26,7 @@ BANKS = 8
 ORDER = (2, 3, 4, 0, 1)
 ROW = {2: 0, 3: 0, 4: 12, 0: 4, 1: 8}
 MOVED_PASS = 4
-MOVED_ROWS = 112
+MOVED_ROWS = 100
 LAST_QUADRANT = 96
 
 HALF = 512

@@ -21,13 +21,14 @@ PASSES = K // 512
 FP8_PASSES = 2
 FP4_PASSES = PASSES - FP8_PASSES
 FLOPS = 2 * K * N * S
-BANKS = 8
 
 ORDER = (2, 3, 4, 0, 1)
 ROW = {2: 0, 3: 0, 4: 12, 0: 4, 1: 8}
 MOVED_PASS = 4
 MOVED_ROWS = 100
 LAST_QUADRANT = 96
+JOINED_GROUP = 1
+SPARE = 112
 
 HALF = 512
 HALVES = ((0, HALF), (HALF, T))
@@ -59,22 +60,28 @@ def tile_moe_pln_lin_none_kernel(tc, xT, w8_words, w8_scales, w4_words, w4_scale
         w4s = keep.tile([P, E * FP4_PASSES, N], U8, name="w4s", align_bytes=64)
         w8s = keep.tile([P, E * FP8_PASSES, N], U8, name="w8s", align_bytes=64)
         moved = [keep.tile([P, GROUP_SLOTS], U8, name=f"moved{g}", align_bytes=64) for g in range(GROUPS)]
-        for t in (first_plane[:], planes[:], w4s[:].rearrange("p x n -> p (x n)"), w8s[:].rearrange("p x n -> p (x n)")):
+        moved_first = keep.tile([P, GROUP_SLOTS], U8, name="moved_first", align_bytes=64)
+        joined = keep.tile([P, T], U8, name="joined", tag="joined", align_bytes=64)
+        for t in (first_plane[:], planes[:], moved_first[:], w4s[:].rearrange("p x n -> p (x n)"), w8s[:].rearrange("p x n -> p (x n)")):
             nc.vector.memset(t.bitcast(I32), 0)
         for t in moved:
             nc.vector.memset(t[LAST_QUADRANT:P, :].bitcast(I32), 0)
 
         x_view = xT.rearrange("(a p j) t -> a p j t", p=P, j=4)
         raw = {}
-        for a, pieces in zip(ORDER, LOADS):
+
+        def load_pass(a):
             raw[a] = []
-            for lo, hi in pieces:
+            for lo, hi in LOADS[ORDER.index(a)]:
                 part = keep.tile([P, 4, hi - lo], F32, name=f"raw{a}_{lo}", align_bytes=64)
                 nc.sync.dma_start(part[:], x_view[a][:, :, lo:hi])
                 raw[a].append((lo, hi, part))
-            if a == first:
-                for tile, source in ((offs_t, offs), (pos1_t, pos1), (pos2_t, pos2)):
-                    nc.sync.dma_start(tile[:], source)
+
+        load_pass(first)
+        for tile, source in ((offs_t, offs), (pos1_t, pos1), (pos2_t, pos2)):
+            nc.sync.dma_start(tile[:], source)
+        load_pass(second)
+        load_pass(third)
 
         w_views = {
             FP8_PASSES: w8_words.rearrange("e a p n r -> p (e a) (n r)"),
@@ -92,15 +99,6 @@ def tile_moe_pln_lin_none_kernel(tc, xT, w8_words, w8_scales, w4_words, w4_scale
         def load_scales(scales, source):
             for r in range(4):
                 nc.sync.dma_start(scales[r:P:32].bitcast(I32), source[:, :, r:16:4, :].rearrange("e a q n -> q (e a) n").bitcast(I32))
-
-        for g in range(GROUPS):
-            load_weights(FP4_PASSES, g, f"fp4_{g}")
-            if g == 0:
-                load_scales(w4s, w4_scales)
-            if g < GROUPS - 1:
-                load_weights(FP8_PASSES, g, f"fp8_{g}")
-            if g == 0:
-                load_scales(w8s, w8_scales)
 
         grouped = {
             (a, lo): keep.tile([P, hi - lo, 4], BF16, name=f"grouped{a}_{lo}", tag=f"grouped{a}_{lo}", align_bytes=64)
@@ -150,8 +148,19 @@ def tile_moe_pln_lin_none_kernel(tc, xT, w8_words, w8_scales, w4_words, w4_scale
             quantise(first, lo, hi)
         for g in range(GROUPS):
             gather_group(f"words{first}", codes[first], U32, g)
-        for g in range(GROUPS - 1):
-            gather_group("first_bytes", first_plane, U8, g)
+        for q in range(4):
+            nc.sync.dma_start(joined[SPARE + 4 * q : SPARE + 4 * q + 4, :].bitcast(I32), first_plane[32 * q : 32 * q + 4, :].bitcast(I32))
+        load_pass(fourth)
+        load_pass(last)
+        for g in range(GROUPS):
+            load_weights(FP4_PASSES, g, f"fp4_{g}")
+            if g == 0:
+                load_scales(w4s, w4_scales)
+            if g < GROUPS - 1:
+                load_weights(FP8_PASSES, g, f"fp8_{g}")
+            if g == 0:
+                load_scales(w8s, w8_scales)
+        gather_group("first_bytes", first_plane, U8, 0)
         prepare(second)
         gather_group("first_bytes", first_plane, U8, GROUPS - 1, behind=second)
         for a, following in ((second, third), (third, fourth)):
@@ -159,27 +168,29 @@ def tile_moe_pln_lin_none_kernel(tc, xT, w8_words, w8_scales, w4_words, w4_scale
                 gather_group(f"words{a}", codes[a], U32, g)
             prepare(following)
             gather_group(f"words{a}", codes[a], U32, GROUPS - 1, behind=following)
+        gather_group(f"words{fourth}", codes[fourth], U32, 0)
         prepare(last)
-        gather_group(f"words{fourth}", codes[fourth], U32, 0, behind=last)
-        late_fourth = keep.tile([P, GROUPS - 1, GROUP_SLOTS], U32, name="late_fourth", tag=f"grouped{last}_0", align_bytes=64)
-
-        def gather_late_fourth(g):
-            slots[f"words{fourth}", g] = late_fourth[:, g - 1, :]
-            gather(late_fourth[:, g - 1, :], codes[fourth], g * GROUP_SLOTS, (g + 1) * GROUP_SLOTS)
+        gather_group(f"words{fourth}", codes[fourth], U32, 1, behind=last)
+        nc.vector.tensor_copy(joined[:SPARE, :].bitcast(I32), planes[:SPARE, :].bitcast(I32))
 
         def gather_bytes(g):
-            gather_group("bytes", planes, U8, g)
+            gather_group("bytes", joined if g == JOINED_GROUP else planes, U8, g)
             rows = slice(ROW[MOVED_PASS], ROW[MOVED_PASS] + MOVED_ROWS)
             nc.sync.dma_start(moved[g][:MOVED_ROWS, :].bitcast(I32), slots["bytes", g][rows, :].bitcast(I32))
+            if g == JOINED_GROUP:
+                for q in range(4):
+                    nc.sync.dma_start(moved_first[32 * q : 32 * q + 4, :].bitcast(I32), slots["bytes", g][SPARE + 4 * q : SPARE + 4 * q + 4, :].bitcast(I32))
+                slots["first_bytes", g] = moved_first[:]
 
         y = keep.tile([P, S], F32, name="y")
-        sums = {}
+        shared = [psum.tile([N, GROUP_SLOTS], F32, name=f"shared{g}") for g in range(GROUPS - 1)]
+        sums = {e: shared[e // GROUP][:, e % GROUP * C : (e % GROUP + 1) * C] for e in range(E - GROUP)}
+        sums.update({e: psum.tile([N, C], F32, name=f"sum{e}")[:] for e in range(E - GROUP, E)})
 
         def multiply(a, experts, start=False, stop=False):
             for e in experts:
                 g, m = divmod(e, GROUP)
-                if start:
-                    sums[e] = psum.tile([N, C], F32, name=f"sum{e}", tag=f"bank{e % BANKS}")
+                alone = g == GROUPS - 1
                 cols = slice(m * C, (m + 1) * C)
                 if a < FP8_PASSES:
                     lhsT = weights[FP8_PASSES, g][:, m * FP8_PASSES + a, :].bitcast(FP8X4)
@@ -194,45 +205,47 @@ def tile_moe_pln_lin_none_kernel(tc, xT, w8_words, w8_scales, w4_words, w4_scale
                 else:
                     rhs_scale = slots["bytes", g][ROW[a] : P, cols]
                 nc.tensor.matmul_mx(
-                    out=sums[e][:], lhsT=lhsT, lhsT_scale=lhsT_scale,
+                    out=sums[e], lhsT=lhsT, lhsT_scale=lhsT_scale,
                     rhs=slots[f"words{a}", g][:, cols].bitcast(FP8X4), rhs_scale=rhs_scale,
-                    start=start, stop=stop,
+                    start=start and (alone or m == 0), stop=stop and (alone or m == GROUP - 1),
                 )
 
         def empty(e, on_vector=False):
             dst = y[:, e * C : (e + 1) * C]
             if on_vector:
-                nc.vector.tensor_copy(dst, sums[e][:])
+                nc.vector.tensor_copy(dst, sums[e])
             else:
-                nc.scalar.copy(dst, sums[e][:])
+                nc.scalar.copy(dst, sums[e])
+
+        def empty_group(g):
+            nc.scalar.copy(y[:, g * GROUP_SLOTS : (g + 1) * GROUP_SLOTS], shared[g][:])
 
         group_a, group_b, group_c = (range(g * GROUP, (g + 1) * GROUP) for g in range(GROUPS))
-        for experts in (group_a, group_b):
+        for experts in (group_a, group_c):
             multiply(first, experts, start=True)
         gather_bytes(0)
         multiply(second, group_a)
-        load_weights(FP8_PASSES, GROUPS - 1, f"words{second}_0")
         gather_bytes(1)
-        gather_group(f"words{last}", codes[last], U32, 0)
+        load_weights(FP8_PASSES, GROUPS - 1, "joined")
         gather_bytes(2)
         gate_t = keep.tile([P, 2, T], F32, name="gate_t", tag="planes", align_bytes=64)
         nc.sync.dma_start(gate_t[:], gate.rearrange("g p t -> p g t"))
+        gather_group(f"words{last}", codes[last], U32, 0)
         multiply(fourth, group_a)
-        multiply(second, group_b)
+        multiply(second, group_b, start=True)
+        multiply(fourth, group_b)
+        multiply(second, group_c)
         multiply(last, group_a)
         multiply(third, group_a, stop=True)
-        for e in group_a:
-            empty(e)
-        gather_late_fourth(1)
+        empty_group(0)
+        late_fourth = keep.tile([P, GROUP_SLOTS], U32, name="late_fourth", tag=f"grouped{last}_0", align_bytes=64)
+        slots[f"words{fourth}", GROUPS - 1] = late_fourth[:]
         gather_group(f"words{last}", codes[last], U32, 1)
+        gather(late_fourth[:], codes[fourth], group_c.start * C, S)
         multiply(third, group_b)
-        multiply(first, group_c, start=True)
-        multiply(second, group_c)
-        multiply(fourth, group_b)
+        multiply(first, group_b)
         multiply(last, group_b, stop=True)
-        for e in group_b:
-            empty(e)
-        gather_late_fourth(2)
+        empty_group(1)
         multiply(third, group_c)
         multiply(fourth, group_c)
         last_slots = keep.tile([P, GROUP_SLOTS], U32, name="last_slots", align_bytes=64)

@@ -59,13 +59,12 @@ def tile_moe_pln_lin_none_kernel(tc, xT, w8_words, w8_scales, w4_words, w4_scale
         planes = keep.tile([P, T], U8, name="planes", tag="planes", align_bytes=64)
         w4s = keep.tile([P, E * FP4_PASSES, N], U8, name="w4s", align_bytes=64)
         w8s = keep.tile([P, E * FP8_PASSES, N], U8, name="w8s", align_bytes=64)
-        moved = [keep.tile([P, GROUP_SLOTS], U8, name=f"moved{g}", align_bytes=64) for g in range(GROUPS)]
+        moved = keep.tile([P, S], U8, name="moved", align_bytes=64)
         moved_first = keep.tile([P, GROUP_SLOTS], U8, name="moved_first", align_bytes=64)
-        joined = keep.tile([P, T], U8, name="joined", tag="joined", align_bytes=64)
+        joined = keep.tile([P, T], U8, name="joined", align_bytes=64)
         for t in (first_plane[:], planes[:], moved_first[:], w4s[:].rearrange("p x n -> p (x n)"), w8s[:].rearrange("p x n -> p (x n)")):
             nc.vector.memset(t.bitcast(I32), 0)
-        for t in moved:
-            nc.vector.memset(t[LAST_QUADRANT:P, :].bitcast(I32), 0)
+        nc.vector.memset(moved[LAST_QUADRANT:P, :].bitcast(I32), 0)
 
         x_view = xT.rearrange("(a p j) t -> a p j t", p=P, j=4)
         raw = {}
@@ -137,10 +136,18 @@ def tile_moe_pln_lin_none_kernel(tc, xT, w8_words, w8_scales, w4_words, w4_scale
 
         slots = {}
 
+        def name_slots(what, tile, lo, hi):
+            for e in range(lo, hi):
+                slots[what, e] = tile[:, (e - lo) * C : (e - lo + 1) * C]
+
+        def gather_run(what, window, dtype, lo, hi, behind=None):
+            tag = f"{what}_{lo}" if behind is None else f"grouped{behind}_{HALF}"
+            tile = keep.tile([P, (hi - lo) * C], dtype, name=f"{what}_{lo}", tag=tag, align_bytes=64)
+            gather(tile[:], window, lo * C, hi * C)
+            name_slots(what, tile, lo, hi)
+
         def gather_group(what, window, dtype, g, behind=None):
-            tag = f"{what}_{g}" if behind is None else f"grouped{behind}_{HALF}"
-            slots[what, g] = keep.tile([P, GROUP_SLOTS], dtype, name=f"{what}_{g}", tag=tag, align_bytes=64)[:]
-            gather(slots[what, g], window, g * GROUP_SLOTS, (g + 1) * GROUP_SLOTS)
+            gather_run(what, window, dtype, g * GROUP, (g + 1) * GROUP, behind)
 
         for (lo, hi), mark in zip(HALVES, VECTOR_CASTS_TO):
             cast(first, lo, mark, on_vector=True)
@@ -161,26 +168,29 @@ def tile_moe_pln_lin_none_kernel(tc, xT, w8_words, w8_scales, w4_words, w4_scale
             if g == 0:
                 load_scales(w8s, w8_scales)
         gather_group("first_bytes", first_plane, U8, 0)
+        gather_run("first_bytes", first_plane, U8, E - GROUP, E - 1)
         prepare(second)
-        gather_group("first_bytes", first_plane, U8, GROUPS - 1, behind=second)
+        gather_run("first_bytes", first_plane, U8, E - 1, E, behind=second)
         for a, following in ((second, third), (third, fourth)):
             for g in range(GROUPS - 1):
                 gather_group(f"words{a}", codes[a], U32, g)
+            gather_run(f"words{a}", codes[a], U32, E - GROUP, E - 1)
             prepare(following)
-            gather_group(f"words{a}", codes[a], U32, GROUPS - 1, behind=following)
+            gather_run(f"words{a}", codes[a], U32, E - 1, E, behind=following)
         gather_group(f"words{fourth}", codes[fourth], U32, 0)
         prepare(last)
         gather_group(f"words{fourth}", codes[fourth], U32, 1, behind=last)
         nc.vector.tensor_copy(joined[:SPARE, :].bitcast(I32), planes[:SPARE, :].bitcast(I32))
 
+        got = keep.tile([P, S], U8, name="got", align_bytes=64)
+
         def gather_bytes(g):
-            gather_group("bytes", joined if g == JOINED_GROUP else planes, U8, g)
-            rows = slice(ROW[MOVED_PASS], ROW[MOVED_PASS] + MOVED_ROWS)
-            nc.sync.dma_start(moved[g][:MOVED_ROWS, :].bitcast(I32), slots["bytes", g][rows, :].bitcast(I32))
+            cols = slice(g * GROUP_SLOTS, (g + 1) * GROUP_SLOTS)
+            gather(got[:, cols], joined if g == JOINED_GROUP else planes, cols.start, cols.stop)
             if g == JOINED_GROUP:
                 for q in range(4):
-                    nc.sync.dma_start(moved_first[32 * q : 32 * q + 4, :].bitcast(I32), slots["bytes", g][SPARE + 4 * q : SPARE + 4 * q + 4, :].bitcast(I32))
-                slots["first_bytes", g] = moved_first[:]
+                    nc.sync.dma_start(moved_first[32 * q : 32 * q + 4, :].bitcast(I32), got[SPARE + 4 * q : SPARE + 4 * q + 4, cols].bitcast(I32))
+                name_slots("first_bytes", moved_first, g * GROUP, (g + 1) * GROUP)
 
         y = keep.tile([P, S], F32, name="y")
         shared = [psum.tile([N, GROUP_SLOTS], F32, name=f"shared{g}") for g in range(GROUPS - 1)]
@@ -191,22 +201,22 @@ def tile_moe_pln_lin_none_kernel(tc, xT, w8_words, w8_scales, w4_words, w4_scale
             for e in experts:
                 g, m = divmod(e, GROUP)
                 alone = g == GROUPS - 1
-                cols = slice(m * C, (m + 1) * C)
                 if a < FP8_PASSES:
-                    lhsT = weights[FP8_PASSES, g][:, m * FP8_PASSES + a, :].bitcast(FP8X4)
+                    words = late_weights[a][:, m, :] if alone else weights[FP8_PASSES, g][:, m * FP8_PASSES + a, :]
+                    lhsT = words.bitcast(FP8X4)
                     lhsT_scale = w8s[:, e * FP8_PASSES + a, :]
                 else:
                     lhsT = weights[FP4_PASSES, g][:, m * FP4_PASSES + a - FP8_PASSES, :].bitcast(FP4X4)
                     lhsT_scale = w4s[:, e * FP4_PASSES + a - FP8_PASSES, :]
                 if a == first:
-                    rhs_scale = slots["first_bytes", g][:, cols]
+                    rhs_scale = slots["first_bytes", e]
                 elif a == MOVED_PASS:
-                    rhs_scale = moved[g][:, cols]
+                    rhs_scale = moved[:, e * C : (e + 1) * C]
                 else:
-                    rhs_scale = slots["bytes", g][ROW[a] : P, cols]
+                    rhs_scale = got[ROW[a] : P, e * C : (e + 1) * C]
                 nc.tensor.matmul_mx(
                     out=sums[e], lhsT=lhsT, lhsT_scale=lhsT_scale,
-                    rhs=slots[f"words{a}", g][:, cols].bitcast(FP8X4), rhs_scale=rhs_scale,
+                    rhs=slots[f"words{a}", e].bitcast(FP8X4), rhs_scale=rhs_scale,
                     start=start and (alone or m == 0), stop=stop and (alone or m == GROUP - 1),
                 )
 
@@ -226,8 +236,13 @@ def tile_moe_pln_lin_none_kernel(tc, xT, w8_words, w8_scales, w4_words, w4_scale
         gather_bytes(0)
         multiply(second, group_a)
         gather_bytes(1)
-        load_weights(FP8_PASSES, GROUPS - 1, "joined")
         gather_bytes(2)
+        nc.sync.dma_start(moved[:MOVED_ROWS, :].bitcast(I32), got[ROW[MOVED_PASS] : ROW[MOVED_PASS] + MOVED_ROWS, :].bitcast(I32))
+        late_weights = {}
+        for a in (fourth, last):
+            late_weights[a] = keep.tile([P, GROUP, 4 * N], U8, name=f"late_weights{a}", align_bytes=64)
+            rows = slice((E - GROUP) * FP8_PASSES + a, E * FP8_PASSES, FP8_PASSES)
+            nc.sync.dma_start(late_weights[a][:].bitcast(I32), w_views[FP8_PASSES][:, rows, :].bitcast(I32))
         gate_t = keep.tile([P, 2, T], F32, name="gate_t", tag="planes", align_bytes=64)
         nc.sync.dma_start(gate_t[:], gate.rearrange("g p t -> p g t"))
         gather_group(f"words{last}", codes[last], U32, 0)
@@ -236,22 +251,20 @@ def tile_moe_pln_lin_none_kernel(tc, xT, w8_words, w8_scales, w4_words, w4_scale
         multiply(fourth, group_b)
         multiply(second, group_c)
         multiply(last, group_a)
+        multiply(first, group_b)
         multiply(third, group_a, stop=True)
         empty_group(0)
         late_fourth = keep.tile([P, GROUP_SLOTS], U32, name="late_fourth", tag=f"grouped{last}_0", align_bytes=64)
-        slots[f"words{fourth}", GROUPS - 1] = late_fourth[:]
+        name_slots(f"words{fourth}", late_fourth, group_c.start, E)
         gather_group(f"words{last}", codes[last], U32, 1)
         gather(late_fourth[:], codes[fourth], group_c.start * C, S)
-        multiply(third, group_b)
-        multiply(first, group_b)
-        multiply(last, group_b, stop=True)
+        multiply(last, group_b)
+        multiply(third, group_b, stop=True)
         empty_group(1)
         multiply(third, group_c)
         multiply(fourth, group_c)
-        last_slots = keep.tile([P, GROUP_SLOTS], U32, name="last_slots", align_bytes=64)
-        slots[f"words{last}", GROUPS - 1] = last_slots[:]
         for lo, hi in LAST_RUNS:
-            gather(last_slots[:, (lo - group_c.start) * C : (hi - group_c.start) * C], codes[last], lo * C, hi * C)
+            gather_run(f"words{last}", codes[last], U32, lo, hi)
             multiply(last, range(lo, hi), stop=True)
             for e in range(lo, hi):
                 empty(e, on_vector=(e == E - 2))

@@ -86,14 +86,14 @@ def tile_moe_pln_lin_none_kernel(tc, xT, w8_words, w8_scales, w4_words, w4_scale
             FP8_PASSES: w8_words.rearrange("e a p n r -> p (e a) (n r)"),
             FP4_PASSES: w4_words.rearrange("e a p b -> p (e a) b"),
         }
-        w_bytes = {FP8_PASSES: GROUP * FP8_PASSES * 4 * N, FP4_PASSES: GROUP * FP4_PASSES * 2 * N}
         weights = {}
 
-        def load_weights(passes, g, tag):
-            tile = keep.tile([P, w_bytes[passes]], U8, name=f"weights{passes}_{g}", tag=tag, align_bytes=64)
-            rows = tile[:].rearrange("p (x b) -> p x b", x=GROUP * passes)
-            nc.sync.dma_start(rows.bitcast(I32), w_views[passes][:, GROUP * passes * g : GROUP * passes * (g + 1), :].bitcast(I32))
-            weights[passes, g] = rows
+        def load_weights(a, lo, hi):
+            passes, index, width = (FP8_PASSES, a, 4 * N) if a < FP8_PASSES else (FP4_PASSES, a - FP8_PASSES, 2 * N)
+            tile = keep.tile([P, hi - lo, width], U8, name=f"weights{a}_{lo}", align_bytes=64)
+            nc.sync.dma_start(tile[:].bitcast(I32), w_views[passes][:, lo * passes + index : hi * passes : passes, :].bitcast(I32))
+            for e in range(lo, hi):
+                weights[a, e] = tile[:, e - lo, :]
 
         def load_scales(scales, source):
             for r in range(4):
@@ -159,14 +159,13 @@ def tile_moe_pln_lin_none_kernel(tc, xT, w8_words, w8_scales, w4_words, w4_scale
             nc.sync.dma_start(joined[SPARE + 4 * q : SPARE + 4 * q + 4, :].bitcast(I32), first_plane[32 * q : 32 * q + 4, :].bitcast(I32))
         load_pass(fourth)
         load_pass(last)
-        for g in range(GROUPS):
-            load_weights(FP4_PASSES, g, f"fp4_{g}")
-            if g == 0:
-                load_scales(w4s, w4_scales)
-            if g < GROUPS - 1:
-                load_weights(FP8_PASSES, g, f"fp8_{g}")
-            if g == 0:
-                load_scales(w8s, w8_scales)
+        load_weights(first, 0, E)
+        load_scales(w4s, w4_scales)
+        load_weights(second, 0, E)
+        load_scales(w8s, w8_scales)
+        load_weights(fourth, 0, E - GROUP)
+        load_weights(last, 0, E - GROUP)
+        load_weights(third, 0, E)
         gather_group("first_bytes", first_plane, U8, 0)
         gather_run("first_bytes", first_plane, U8, E - GROUP, E - 1)
         prepare(second)
@@ -202,11 +201,10 @@ def tile_moe_pln_lin_none_kernel(tc, xT, w8_words, w8_scales, w4_words, w4_scale
                 g, m = divmod(e, GROUP)
                 alone = g == GROUPS - 1
                 if a < FP8_PASSES:
-                    words = late_weights[a][:, m, :] if alone else weights[FP8_PASSES, g][:, m * FP8_PASSES + a, :]
-                    lhsT = words.bitcast(FP8X4)
+                    lhsT = weights[a, e].bitcast(FP8X4)
                     lhsT_scale = w8s[:, e * FP8_PASSES + a, :]
                 else:
-                    lhsT = weights[FP4_PASSES, g][:, m * FP4_PASSES + a - FP8_PASSES, :].bitcast(FP4X4)
+                    lhsT = weights[a, e].bitcast(FP4X4)
                     lhsT_scale = w4s[:, e * FP4_PASSES + a - FP8_PASSES, :]
                 if a == first:
                     rhs_scale = slots["first_bytes", e]
@@ -238,11 +236,8 @@ def tile_moe_pln_lin_none_kernel(tc, xT, w8_words, w8_scales, w4_words, w4_scale
         gather_bytes(1)
         gather_bytes(2)
         nc.sync.dma_start(moved[:MOVED_ROWS, :].bitcast(I32), got[ROW[MOVED_PASS] : ROW[MOVED_PASS] + MOVED_ROWS, :].bitcast(I32))
-        late_weights = {}
         for a in (fourth, last):
-            late_weights[a] = keep.tile([P, GROUP, 4 * N], U8, name=f"late_weights{a}", align_bytes=64)
-            rows = slice((E - GROUP) * FP8_PASSES + a, E * FP8_PASSES, FP8_PASSES)
-            nc.sync.dma_start(late_weights[a][:].bitcast(I32), w_views[FP8_PASSES][:, rows, :].bitcast(I32))
+            load_weights(a, E - GROUP, E)
         gate_t = keep.tile([P, 2, T], F32, name="gate_t", tag="planes", align_bytes=64)
         nc.sync.dma_start(gate_t[:], gate.rearrange("g p t -> p g t"))
         gather_group(f"words{last}", codes[last], U32, 0)

@@ -1,6 +1,7 @@
 from contextlib import ExitStack
 
 import concourse.mybir as mybir
+from concourse.masks import make_identity
 
 F32 = mybir.dt.float32
 BF16 = mybir.dt.bfloat16
@@ -56,7 +57,7 @@ def tile_moe_pln_lin_none_kernel(tc, xT, w8_words, w8_scales, w4_words, w4_scale
         pos2_t = keep.tile([P, T // 16], U16, name="pos2_t")
 
         first_plane = keep.tile([P, T], U8, name="first_plane", align_bytes=64)
-        planes = keep.tile([P, T], U8, name="planes", tag="planes", align_bytes=64)
+        planes = keep.tile([P, T], U8, name="planes", align_bytes=64)
         w4s = keep.tile([P, E * FP4_PASSES, N], U8, name="w4s", align_bytes=64)
         w8s = keep.tile([P, E * FP8_PASSES, N], U8, name="w8s", align_bytes=64)
         moved = keep.tile([P, S], U8, name="moved", align_bytes=64)
@@ -72,7 +73,7 @@ def tile_moe_pln_lin_none_kernel(tc, xT, w8_words, w8_scales, w4_words, w4_scale
         def load_pass(a):
             raw[a] = []
             for lo, hi in LOADS[ORDER.index(a)]:
-                part = keep.tile([P, 4, hi - lo], F32, name=f"raw{a}_{lo}", align_bytes=64)
+                part = keep.tile([P, 4, hi - lo], F32, name=f"raw{a}_{lo}", tag=f"raw{a}_{lo}", align_bytes=64)
                 nc.sync.dma_start(part[:], x_view[a][:, :, lo:hi])
                 raw[a].append((lo, hi, part))
 
@@ -81,6 +82,20 @@ def tile_moe_pln_lin_none_kernel(tc, xT, w8_words, w8_scales, w4_words, w4_scale
             nc.sync.dma_start(tile[:], source)
         load_pass(second)
         load_pass(third)
+
+        identity = keep.tile([P, P], F32, name="identity")
+        make_identity(nc, identity[:])
+        spread = {}
+        for lo, hi in HALVES:
+            width = (hi - lo) // P
+            row = keep.tile([P, 2, width], F32, name=f"gate_row{lo}")
+            nc.sync.dma_start(row[:], gate[:, 0, lo:hi].rearrange("c (n m) -> n c m", m=width))
+            for choices in ((0,), (1,)) if lo == 0 else ((0, 1),):
+                bank = psum.tile([P, len(choices), width, P], F32, name=f"spread{lo}_{choices[0]}", tag=f"spread{choices[0]}" if lo == 0 else "shared1")
+                for j, choice in enumerate(choices):
+                    for m in range(width):
+                        nc.tensor.transpose(bank[:, j, m, :], row[:, choice, m : m + 1].to_broadcast([P, P]), identity[:])
+                spread[lo, hi, choices] = bank
 
         w_views = {
             FP8_PASSES: w8_words.rearrange("e a p n r -> p (e a) (n r)"),
@@ -179,6 +194,10 @@ def tile_moe_pln_lin_none_kernel(tc, xT, w8_words, w8_scales, w4_words, w4_scale
         gather_group(f"words{fourth}", codes[fourth], U32, 0)
         prepare(last)
         gather_group(f"words{fourth}", codes[fourth], U32, 1, behind=last)
+        gate_t = keep.tile([P, 2, T], F32, name="gate_t", tag=f"raw{last}_0", align_bytes=64)
+        for (lo, hi, choices), bank in spread.items():
+            dst = gate_t[:, choices[0] : choices[-1] + 1, lo:hi].rearrange("p c (n m) -> p c n m", n=P)
+            nc.scalar.copy(dst, bank[:].rearrange("p c m n -> p c n m"))
         nc.vector.tensor_copy(joined[:SPARE, :].bitcast(I32), planes[:SPARE, :].bitcast(I32))
 
         got = keep.tile([P, S], U8, name="got", align_bytes=64)
@@ -192,7 +211,7 @@ def tile_moe_pln_lin_none_kernel(tc, xT, w8_words, w8_scales, w4_words, w4_scale
                 name_slots("first_bytes", moved_first, g * GROUP, (g + 1) * GROUP)
 
         y = keep.tile([P, S], F32, name="y")
-        shared = [psum.tile([N, GROUP_SLOTS], F32, name=f"shared{g}") for g in range(GROUPS - 1)]
+        shared = [psum.tile([N, GROUP_SLOTS], F32, name=f"shared{g}", tag=f"shared{g}") for g in range(GROUPS - 1)]
         sums = {e: shared[e // GROUP][:, e % GROUP * C : (e % GROUP + 1) * C] for e in range(E - GROUP)}
         sums.update({e: psum.tile([N, C], F32, name=f"sum{e}")[:] for e in range(E - GROUP, E)})
 
@@ -238,8 +257,6 @@ def tile_moe_pln_lin_none_kernel(tc, xT, w8_words, w8_scales, w4_words, w4_scale
         nc.sync.dma_start(moved[:MOVED_ROWS, :].bitcast(I32), got[ROW[MOVED_PASS] : ROW[MOVED_PASS] + MOVED_ROWS, :].bitcast(I32))
         for a in (fourth, last):
             load_weights(a, E - GROUP, E)
-        gate_t = keep.tile([P, 2, T], F32, name="gate_t", tag="planes", align_bytes=64)
-        nc.sync.dma_start(gate_t[:], gate.rearrange("g p t -> p g t"))
         gather_group(f"words{last}", codes[last], U32, 0)
         multiply(fourth, group_a)
         multiply(second, group_b, start=True)

@@ -25,6 +25,7 @@ FLOPS = 2 * K * N * S
 
 ORDER = (2, 3, 4, 0, 1)
 ROW = {2: 0, 3: 0, 4: 12, 0: 4, 1: 8}
+FP8_SCALE_ROW = 8
 MOVED_PASS = 4
 MOVED_ROWS = 100
 LAST_QUADRANT = 96
@@ -41,6 +42,7 @@ LAST_CAST = 16
 GROUP = 4
 GROUPS = E // GROUP
 GROUP_SLOTS = GROUP * C
+GATE_ROWS = 2 * T // P
 LAST_RUNS = ((8, 10), (10, 11), (11, 12))
 OUT_PIECES = ((0, 256, True), (256, 448, False), (448, 640, True), (640, T, True))
 
@@ -78,24 +80,17 @@ def tile_moe_pln_lin_none_kernel(tc, xT, w8_words, w8_scales, w4_words, w4_scale
                 raw[a].append((lo, hi, part))
 
         load_pass(first)
-        for tile, source in ((offs_t, offs), (pos1_t, pos1), (pos2_t, pos2)):
-            nc.sync.dma_start(tile[:], source)
+        nc.sync.dma_start(offs_t[:], offs)
         load_pass(second)
         load_pass(third)
 
         identity = keep.tile([P, P], F32, name="identity")
         make_identity(nc, identity[:])
-        spread = {}
-        for lo, hi in HALVES:
-            width = (hi - lo) // P
-            row = keep.tile([P, 2, width], F32, name=f"gate_row{lo}")
-            nc.sync.dma_start(row[:], gate[:, 0, lo:hi].rearrange("c (n m) -> n c m", m=width))
-            for choices in ((0,), (1,)) if lo == 0 else ((0, 1),):
-                bank = psum.tile([P, len(choices), width, P], F32, name=f"spread{lo}_{choices[0]}", tag=f"spread{choices[0]}" if lo == 0 else "shared1")
-                for j, choice in enumerate(choices):
-                    for m in range(width):
-                        nc.tensor.transpose(bank[:, j, m, :], row[:, choice, m : m + 1].to_broadcast([P, P]), identity[:])
-                spread[lo, hi, choices] = bank
+        gate_rows = keep.tile([P, P], F32, name="gate_rows")
+        nc.gpsimd.memset(gate_rows[:], 0.0)
+        both = gate.rearrange("c r (m n) -> (c r m) n", n=P)
+        nc.sync.dma_start(gate_rows[:GATE_ROWS, :], both[(N - 1) * T // P : (N + 1) * T // P, :])
+
 
         w_views = {
             FP8_PASSES: w8_words.rearrange("e a p n r -> p (e a) (n r)"),
@@ -110,9 +105,9 @@ def tile_moe_pln_lin_none_kernel(tc, xT, w8_words, w8_scales, w4_words, w4_scale
             for e in range(lo, hi):
                 weights[a, e] = tile[:, e - lo, :]
 
-        def load_scales(scales, source):
+        def load_scales(scales, source, row):
             for r in range(4):
-                nc.sync.dma_start(scales[r:P:32].bitcast(I32), source[:, :, r:16:4, :].rearrange("e a q n -> q (e a) n").bitcast(I32))
+                nc.sync.dma_start(scales[row + r : P : 32].bitcast(I32), source[:, :, r:16:4, :].rearrange("e a q n -> q (e a) n").bitcast(I32))
 
         grouped = {
             (a, lo): keep.tile([P, hi - lo, 4], BF16, name=f"grouped{a}_{lo}", tag=f"grouped{a}_{lo}", align_bytes=64)
@@ -175,9 +170,9 @@ def tile_moe_pln_lin_none_kernel(tc, xT, w8_words, w8_scales, w4_words, w4_scale
         load_pass(fourth)
         load_pass(last)
         load_weights(first, 0, E)
-        load_scales(w4s, w4_scales)
+        load_scales(w4s, w4_scales, 0)
         load_weights(second, 0, E)
-        load_scales(w8s, w8_scales)
+        load_scales(w8s, w8_scales, FP8_SCALE_ROW)
         load_weights(fourth, 0, E - GROUP)
         load_weights(last, 0, E - GROUP)
         load_weights(third, 0, E)
@@ -194,10 +189,17 @@ def tile_moe_pln_lin_none_kernel(tc, xT, w8_words, w8_scales, w4_words, w4_scale
         gather_group(f"words{fourth}", codes[fourth], U32, 0)
         prepare(last)
         gather_group(f"words{fourth}", codes[fourth], U32, 1, behind=last)
-        gate_t = keep.tile([P, 2, T], F32, name="gate_t", tag=f"raw{last}_0", align_bytes=64)
-        for (lo, hi, choices), bank in spread.items():
-            dst = gate_t[:, choices[0] : choices[-1] + 1, lo:hi].rearrange("p c (n m) -> p c n m", n=P)
-            nc.scalar.copy(dst, bank[:].rearrange("p c m n -> p c n m"))
+        turned = psum.tile([P, P], F32, name="turned", tag="shared0")
+        nc.tensor.transpose(turned[:], gate_rows[:], identity[:])
+        gate_columns = keep.tile([P, GATE_ROWS], F32, name="gate_columns", tag=f"raw{last}_0", align_bytes=64)
+        nc.scalar.copy(gate_columns[:], turned[:, :GATE_ROWS])
+        gate_t = keep.tile([P, 2, T], F32, name="gate_t")
+        for b, tag in enumerate(("spread0", "spread1", "shared1")):
+            bank = psum.tile([P, GROUP, P], F32, name=f"spread{b}", tag=tag)
+            for m in range(GROUP):
+                column = gate_columns[:, GROUP * b + m : GROUP * b + m + 1]
+                nc.tensor.transpose(bank[:, m, :], column.to_broadcast([P, P]), identity[:])
+            nc.scalar.copy(gate_t[:].rearrange("p c t -> p (c t)")[:, b * GROUP * P : (b + 1) * GROUP * P], bank[:].rearrange("p m n -> p (m n)"))
         nc.vector.tensor_copy(joined[:SPARE, :].bitcast(I32), planes[:SPARE, :].bitcast(I32))
 
         got = keep.tile([P, S], U8, name="got", align_bytes=64)
@@ -221,7 +223,7 @@ def tile_moe_pln_lin_none_kernel(tc, xT, w8_words, w8_scales, w4_words, w4_scale
                 alone = g == GROUPS - 1
                 if a < FP8_PASSES:
                     lhsT = weights[a, e].bitcast(FP8X4)
-                    lhsT_scale = w8s[:, e * FP8_PASSES + a, :]
+                    lhsT_scale = w8s[FP8_SCALE_ROW:P, e * FP8_PASSES + a, :]
                 else:
                     lhsT = weights[a, e].bitcast(FP4X4)
                     lhsT_scale = w4s[:, e * FP4_PASSES + a - FP8_PASSES, :]
@@ -257,6 +259,8 @@ def tile_moe_pln_lin_none_kernel(tc, xT, w8_words, w8_scales, w4_words, w4_scale
         nc.sync.dma_start(moved[:MOVED_ROWS, :].bitcast(I32), got[ROW[MOVED_PASS] : ROW[MOVED_PASS] + MOVED_ROWS, :].bitcast(I32))
         for a in (fourth, last):
             load_weights(a, E - GROUP, E)
+        for tile, source in ((pos1_t, pos1), (pos2_t, pos2)):
+            nc.sync.dma_start(tile[:], source)
         gather_group(f"words{last}", codes[last], U32, 0)
         multiply(fourth, group_a)
         multiply(second, group_b, start=True)

@@ -29,7 +29,7 @@ FP8_SCALE_ROW = 8
 MOVED_PASS = 4
 MOVED_ROWS = 100
 LAST_QUADRANT = 96
-JOINED_GROUP = 1
+JOINED = 6
 SPARE = 112
 
 HALF = 512
@@ -63,7 +63,7 @@ def tile_moe_pln_lin_none_kernel(tc, xT, w8_words, w8_scales, w4_words, w4_scale
         w4s = keep.tile([P, E * FP4_PASSES, N], U8, name="w4s", align_bytes=64)
         w8s = keep.tile([P, E * FP8_PASSES, N], U8, name="w8s", align_bytes=64)
         moved = keep.tile([P, S], U8, name="moved", align_bytes=64)
-        moved_first = keep.tile([P, GROUP_SLOTS], U8, name="moved_first", align_bytes=64)
+        moved_first = keep.tile([P, JOINED * C], U8, name="moved_first", align_bytes=64)
         joined = keep.tile([P, T], U8, name="joined", align_bytes=64)
         for t in (first_plane[:], planes[:], moved_first[:], w4s[:].rearrange("p x n -> p (x n)"), w8s[:].rearrange("p x n -> p (x n)")):
             nc.vector.memset(t.bitcast(I32), 0)
@@ -176,7 +176,7 @@ def tile_moe_pln_lin_none_kernel(tc, xT, w8_words, w8_scales, w4_words, w4_scale
         load_weights(fourth, 0, E - GROUP)
         load_weights(last, 0, E - GROUP)
         load_weights(third, 0, E)
-        gather_group("first_bytes", first_plane, U8, 0)
+        gather_run("first_bytes", first_plane, U8, JOINED, E - GROUP)
         gather_run("first_bytes", first_plane, U8, E - GROUP, E - 1)
         prepare(second)
         gather_run("first_bytes", first_plane, U8, E - 1, E, behind=second)
@@ -188,7 +188,7 @@ def tile_moe_pln_lin_none_kernel(tc, xT, w8_words, w8_scales, w4_words, w4_scale
             gather_run(f"words{a}", codes[a], U32, E - 1, E, behind=following)
         gather_group(f"words{fourth}", codes[fourth], U32, 0)
         prepare(last)
-        gather_group(f"words{fourth}", codes[fourth], U32, 1, behind=last)
+        gather_run(f"words{fourth}", codes[fourth], U32, GROUP, GROUP + 1, behind=last)
         turned = psum.tile([P, P], F32, name="turned", tag="shared0")
         nc.tensor.transpose(turned[:], gate_rows[:], identity[:])
         gate_columns = keep.tile([P, GATE_ROWS], F32, name="gate_columns", tag=f"raw{last}_0", align_bytes=64)
@@ -202,15 +202,25 @@ def tile_moe_pln_lin_none_kernel(tc, xT, w8_words, w8_scales, w4_words, w4_scale
             nc.scalar.copy(gate_t[:].rearrange("p c t -> p (c t)")[:, b * GROUP * P : (b + 1) * GROUP * P], bank[:].rearrange("p m n -> p (m n)"))
         nc.vector.tensor_copy(joined[:SPARE, :].bitcast(I32), planes[:SPARE, :].bitcast(I32))
 
-        got = keep.tile([P, S], U8, name="got", align_bytes=64)
+        late_fourth = keep.tile([P, (E - GROUP - 1) * C], U32, name="late_fourth", tag=f"grouped{last}_0", align_bytes=64)
+        name_slots(f"words{fourth}", late_fourth, GROUP + 1, E)
 
-        def gather_bytes(g):
-            cols = slice(g * GROUP_SLOTS, (g + 1) * GROUP_SLOTS)
-            gather(got[:, cols], joined if g == JOINED_GROUP else planes, cols.start, cols.stop)
-            if g == JOINED_GROUP:
-                for q in range(4):
-                    nc.sync.dma_start(moved_first[32 * q : 32 * q + 4, :].bitcast(I32), got[SPARE + 4 * q : SPARE + 4 * q + 4, cols].bitcast(I32))
-                name_slots("first_bytes", moved_first, g * GROUP, (g + 1) * GROUP)
+        def gather_late(lo, hi):
+            gather(late_fourth[:, (lo - GROUP - 1) * C : (hi - GROUP - 1) * C], codes[fourth], lo * C, hi * C)
+
+        gather_late(GROUP + 1, GROUP + 2)
+        got = keep.tile([P, S], U8, name="got", align_bytes=64)
+        for g in range(GROUPS - 1):
+            gather(got[:, g * GROUP_SLOTS : (g + 1) * GROUP_SLOTS], joined, g * GROUP_SLOTS, (g + 1) * GROUP_SLOTS)
+        for q in range(4):
+            nc.sync.dma_start(moved_first[32 * q : 32 * q + 4, :].bitcast(I32), got[SPARE + 4 * q : SPARE + 4 * q + 4, : JOINED * C].bitcast(I32))
+        name_slots("first_bytes", moved_first, 0, JOINED)
+        gather(got[:, S - GROUP_SLOTS :], planes, S - GROUP_SLOTS, S)
+        nc.sync.dma_start(moved[:MOVED_ROWS, :].bitcast(I32), got[ROW[MOVED_PASS] : ROW[MOVED_PASS] + MOVED_ROWS, :].bitcast(I32))
+        for a in (fourth, last):
+            load_weights(a, E - GROUP, E)
+        for tile, source in ((pos1_t, pos1), (pos2_t, pos2)):
+            nc.sync.dma_start(tile[:], source)
 
         y = keep.tile([P, S], F32, name="y")
         shared = [psum.tile([N, GROUP_SLOTS], F32, name=f"shared{g}", tag=f"shared{g}") for g in range(GROUPS - 1)]
@@ -236,7 +246,7 @@ def tile_moe_pln_lin_none_kernel(tc, xT, w8_words, w8_scales, w4_words, w4_scale
                 nc.tensor.matmul_mx(
                     out=sums[e], lhsT=lhsT, lhsT_scale=lhsT_scale,
                     rhs=slots[f"words{a}", e].bitcast(FP8X4), rhs_scale=rhs_scale,
-                    start=start and (alone or m == 0), stop=stop and (alone or m == GROUP - 1),
+                    start=start and (alone or e == experts.start), stop=stop and (alone or m == GROUP - 1),
                 )
 
         def empty(e, on_vector=False):
@@ -250,31 +260,22 @@ def tile_moe_pln_lin_none_kernel(tc, xT, w8_words, w8_scales, w4_words, w4_scale
             nc.scalar.copy(y[:, g * GROUP_SLOTS : (g + 1) * GROUP_SLOTS], shared[g][:])
 
         group_a, group_b, group_c = (range(g * GROUP, (g + 1) * GROUP) for g in range(GROUPS))
-        for experts in (group_a, group_c):
-            multiply(first, experts, start=True)
-        gather_bytes(0)
-        multiply(second, group_a)
-        gather_bytes(1)
-        gather_bytes(2)
-        nc.sync.dma_start(moved[:MOVED_ROWS, :].bitcast(I32), got[ROW[MOVED_PASS] : ROW[MOVED_PASS] + MOVED_ROWS, :].bitcast(I32))
-        for a in (fourth, last):
-            load_weights(a, E - GROUP, E)
-        for tile, source in ((pos1_t, pos1), (pos2_t, pos2)):
-            nc.sync.dma_start(tile[:], source)
-        gather_group(f"words{last}", codes[last], U32, 0)
+        multiply(first, group_c, start=True)
+        multiply(first, range(JOINED, E - GROUP), start=True)
+        multiply(second, group_a, start=True)
         multiply(fourth, group_a)
-        multiply(second, group_b, start=True)
-        multiply(fourth, group_b)
+        multiply(second, group_b)
         multiply(second, group_c)
+        gather_late(GROUP + 2, E - GROUP)
+        multiply(fourth, group_b)
+        gather_group(f"words{last}", codes[last], U32, 0)
         multiply(last, group_a)
-        multiply(first, group_b)
+        multiply(first, range(JOINED))
+        gather_group(f"words{last}", codes[last], U32, 1)
+        multiply(last, group_b)
+        gather_late(E - GROUP, E)
         multiply(third, group_a, stop=True)
         empty_group(0)
-        late_fourth = keep.tile([P, GROUP_SLOTS], U32, name="late_fourth", tag=f"grouped{last}_0", align_bytes=64)
-        name_slots(f"words{fourth}", late_fourth, group_c.start, E)
-        gather_group(f"words{last}", codes[last], U32, 1)
-        gather(late_fourth[:], codes[fourth], group_c.start * C, S)
-        multiply(last, group_b)
         multiply(third, group_b, stop=True)
         empty_group(1)
         multiply(third, group_c)

@@ -42,6 +42,8 @@ LAST_CAST = 16
 GROUP = 4
 GROUPS = E // GROUP
 GROUP_SLOTS = GROUP * C
+WIDE = 2048
+WIDE_BYTES = 1024
 GATE_ROWS = 2 * T // P
 LAST_RUNS = ((8, 10), (10, 11), (11, 12))
 OUT_PIECES = ((0, 256, True), (256, 448, False), (448, 640, True), (640, T, True))
@@ -58,15 +60,15 @@ def tile_moe_pln_lin_none_kernel(tc, xT, w8_words, w8_scales, w4_words, w4_scale
         pos1_t = keep.tile([P, T // 16], U16, name="pos1_t")
         pos2_t = keep.tile([P, T // 16], U16, name="pos2_t")
 
-        first_plane = keep.tile([P, T], U8, name="first_plane", align_bytes=64)
+        first_plane = keep.tile([P, WIDE_BYTES], U8, name="first_plane", align_bytes=64)
         planes = keep.tile([P, T], U8, name="planes", align_bytes=64)
-        w4s = keep.tile([P, E * FP4_PASSES, N], U8, name="w4s", align_bytes=64)
-        w8s = keep.tile([P, E * FP8_PASSES, N], U8, name="w8s", align_bytes=64)
         moved = keep.tile([P, S], U8, name="moved", align_bytes=64)
         moved_first = keep.tile([P, JOINED * C], U8, name="moved_first", align_bytes=64)
         joined = keep.tile([P, T], U8, name="joined", align_bytes=64)
-        for t in (first_plane[:], planes[:], moved_first[:], w4s[:].rearrange("p x n -> p (x n)"), w8s[:].rearrange("p x n -> p (x n)")):
+        for t in (first_plane[:], planes[:], moved_first[:]):
             nc.vector.memset(t.bitcast(I32), 0)
+        all_codes = keep.tile([P, (PASSES - 1) * T + WIDE], U32, name="all_codes", align_bytes=64)
+        nc.vector.memset(all_codes[:, PASSES * T :].bitcast(I32), 0)
         nc.vector.memset(moved[LAST_QUADRANT:P, :].bitcast(I32), 0)
 
         x_view = xT.rearrange("(a p j) t -> a p j t", p=P, j=4)
@@ -114,7 +116,9 @@ def tile_moe_pln_lin_none_kernel(tc, xT, w8_words, w8_scales, w4_words, w4_scale
             for a in ORDER
             for lo, hi in HALVES
         }
-        codes = {a: keep.tile([P, T], U32, name=f"codes{a}", align_bytes=64) for a in ORDER}
+        base_of = {a: (PASSES - 1 - i) * T for i, a in enumerate(ORDER)}
+        codes = {a: all_codes[:, base_of[a] : base_of[a] + T] for a in ORDER}
+        wide = {a: all_codes[:, base_of[a] : base_of[a] + WIDE] for a in ORDER}
 
         def cast(a, lo, hi, on_vector=False):
             piece = 0 if hi <= HALF else HALF
@@ -142,7 +146,7 @@ def tile_moe_pln_lin_none_kernel(tc, xT, w8_words, w8_scales, w4_words, w4_scale
                 quantise(a, lo, hi)
 
         def gather(dst, window, lo, hi):
-            nc.vector.tensor_copy(dst, window[:].indirect(offs_t[:, lo // 16 : hi // 16]))
+            nc.vector.tensor_copy(dst, window.indirect(offs_t[:, lo // 16 : hi // 16]))
 
         slots = {}
 
@@ -163,12 +167,13 @@ def tile_moe_pln_lin_none_kernel(tc, xT, w8_words, w8_scales, w4_words, w4_scale
             cast(first, lo, mark, on_vector=True)
             cast(first, mark, hi)
             quantise(first, lo, hi)
-        for g in range(GROUPS):
-            gather_group(f"words{first}", codes[first], U32, g)
+        gather_run(f"words{first}", wide[first], U32, 0, E)
         for q in range(4):
-            nc.sync.dma_start(joined[SPARE + 4 * q : SPARE + 4 * q + 4, :].bitcast(I32), first_plane[32 * q : 32 * q + 4, :].bitcast(I32))
+            nc.sync.dma_start(joined[SPARE + 4 * q : SPARE + 4 * q + 4, :].bitcast(I32), first_plane[32 * q : 32 * q + 4, :T].bitcast(I32))
         load_pass(fourth)
         load_pass(last)
+        w4s = keep.tile([P, E * FP4_PASSES, N], U8, name="w4s", tag=f"raw{first}_0", align_bytes=64)
+        w8s = keep.tile([P, E * FP8_PASSES, N], U8, name="w8s", tag=f"raw{first}_{HALF}", align_bytes=64)
         load_weights(first, 0, E)
         load_scales(w4s, w4_scales, 0)
         load_weights(second, 0, E)
@@ -176,14 +181,11 @@ def tile_moe_pln_lin_none_kernel(tc, xT, w8_words, w8_scales, w4_words, w4_scale
         load_weights(fourth, 0, E - GROUP)
         load_weights(last, 0, E - GROUP)
         load_weights(third, 0, E)
-        gather_run("first_bytes", first_plane, U8, JOINED, E - GROUP)
-        gather_run("first_bytes", first_plane, U8, E - GROUP, E - 1)
+        gather_run("first_bytes", first_plane[:], U8, JOINED, E - 1)
         prepare(second)
-        gather_run("first_bytes", first_plane, U8, E - 1, E, behind=second)
+        gather_run("first_bytes", first_plane[:], U8, E - 1, E, behind=second)
         for a, following in ((second, third), (third, fourth)):
-            for g in range(GROUPS - 1):
-                gather_group(f"words{a}", codes[a], U32, g)
-            gather_run(f"words{a}", codes[a], U32, E - GROUP, E - 1)
+            gather_run(f"words{a}", wide[a], U32, 0, E - 1)
             prepare(following)
             gather_run(f"words{a}", codes[a], U32, E - 1, E, behind=following)
         gather_group(f"words{fourth}", codes[fourth], U32, 0)
@@ -211,11 +213,11 @@ def tile_moe_pln_lin_none_kernel(tc, xT, w8_words, w8_scales, w4_words, w4_scale
         gather_late(GROUP + 1, GROUP + 2)
         got = keep.tile([P, S], U8, name="got", align_bytes=64)
         for g in range(GROUPS - 1):
-            gather(got[:, g * GROUP_SLOTS : (g + 1) * GROUP_SLOTS], joined, g * GROUP_SLOTS, (g + 1) * GROUP_SLOTS)
+            gather(got[:, g * GROUP_SLOTS : (g + 1) * GROUP_SLOTS], joined[:], g * GROUP_SLOTS, (g + 1) * GROUP_SLOTS)
         for q in range(4):
             nc.sync.dma_start(moved_first[32 * q : 32 * q + 4, :].bitcast(I32), got[SPARE + 4 * q : SPARE + 4 * q + 4, : JOINED * C].bitcast(I32))
         name_slots("first_bytes", moved_first, 0, JOINED)
-        gather(got[:, S - GROUP_SLOTS :], planes, S - GROUP_SLOTS, S)
+        gather(got[:, S - GROUP_SLOTS :], planes[:], S - GROUP_SLOTS, S)
         nc.sync.dma_start(moved[:MOVED_ROWS, :].bitcast(I32), got[ROW[MOVED_PASS] : ROW[MOVED_PASS] + MOVED_ROWS, :].bitcast(I32))
         for a in (fourth, last):
             load_weights(a, E - GROUP, E)

@@ -61,7 +61,7 @@ def tile_moe_pln_lin_none_kernel(tc, xT, w8_words, w8_scales, w4_words, w4_scale
         pos2_t = keep.tile([P, T // 16], U16, name="pos2_t")
 
         first_plane = keep.tile([P, WIDE_BYTES], U8, name="first_plane", align_bytes=64)
-        planes = keep.tile([P, T], U8, name="planes", align_bytes=64)
+        planes = keep.tile([P, T], U8, name="planes", tag="planes", align_bytes=64)
         moved = keep.tile([P, S], U8, name="moved", align_bytes=64)
         moved_first = keep.tile([P, JOINED * C], U8, name="moved_first", align_bytes=64)
         joined = keep.tile([P, T], U8, name="joined", align_bytes=64)
@@ -107,9 +107,10 @@ def tile_moe_pln_lin_none_kernel(tc, xT, w8_words, w8_scales, w4_words, w4_scale
             for e in range(lo, hi):
                 weights[a, e] = tile[:, e - lo, :]
 
-        def load_scales(scales, source, row):
-            for r in range(4):
-                nc.sync.dma_start(scales[row + r : P : 32].bitcast(I32), source[:, :, r:16:4, :].rearrange("e a q n -> q (e a) n").bitcast(I32))
+        def load_scales(rows):
+            for r in rows:
+                for scales, source, row in ((w4s, w4_scales, 0), (w8s, w8_scales, FP8_SCALE_ROW)):
+                    nc.sync.dma_start(scales[row + r : P : 32].bitcast(I32), source[:, :, r:16:4, :].rearrange("e a q n -> q (e a) n").bitcast(I32))
 
         grouped = {
             (a, lo): keep.tile([P, hi - lo, 4], BF16, name=f"grouped{a}_{lo}", tag=f"grouped{a}_{lo}", align_bytes=64)
@@ -175,9 +176,9 @@ def tile_moe_pln_lin_none_kernel(tc, xT, w8_words, w8_scales, w4_words, w4_scale
         w4s = keep.tile([P, E * FP4_PASSES, N], U8, name="w4s", tag=f"raw{first}_0", align_bytes=64)
         w8s = keep.tile([P, E * FP8_PASSES, N], U8, name="w8s", tag=f"raw{first}_{HALF}", align_bytes=64)
         load_weights(first, 0, E)
-        load_scales(w4s, w4_scales, 0)
+        load_scales((0, 1))
         load_weights(second, 0, E)
-        load_scales(w8s, w8_scales, FP8_SCALE_ROW)
+        load_scales((2, 3))
         load_weights(fourth, 0, E - GROUP)
         load_weights(last, 0, E - GROUP)
         load_weights(third, 0, E)
@@ -204,23 +205,31 @@ def tile_moe_pln_lin_none_kernel(tc, xT, w8_words, w8_scales, w4_words, w4_scale
             nc.scalar.copy(gate_t[:].rearrange("p c t -> p (c t)")[:, b * GROUP * P : (b + 1) * GROUP * P], bank[:].rearrange("p m n -> p (m n)"))
         nc.vector.tensor_copy(joined[:SPARE, :].bitcast(I32), planes[:SPARE, :].bitcast(I32))
 
-        late_fourth = keep.tile([P, (E - GROUP - 1) * C], U32, name="late_fourth", tag=f"grouped{last}_0", align_bytes=64)
-        name_slots(f"words{fourth}", late_fourth, GROUP + 1, E)
-
-        def gather_late(lo, hi):
-            gather(late_fourth[:, (lo - GROUP - 1) * C : (hi - GROUP - 1) * C], codes[fourth], lo * C, hi * C)
-
-        gather_late(GROUP + 1, GROUP + 2)
+        between = keep.tile([P, C], U32, name="between", tag=f"grouped{last}_0", align_bytes=64)
+        gather(between[:], codes[fourth], (GROUP + 1) * C, (GROUP + 2) * C)
+        name_slots(f"words{fourth}", between, GROUP + 1, GROUP + 2)
         got = keep.tile([P, S], U8, name="got", align_bytes=64)
-        for g in range(GROUPS - 1):
+        for g in range(GROUPS):
             gather(got[:, g * GROUP_SLOTS : (g + 1) * GROUP_SLOTS], joined[:], g * GROUP_SLOTS, (g + 1) * GROUP_SLOTS)
+        late_words = keep.tile([P, (2 * E - GROUP - 2) * C], U32, name="late_words", tag="planes", align_bytes=64)
+        name_slots(f"words{last}", late_words, 0, E)
+        name_slots(f"words{fourth}", late_words[:, S:], GROUP + 2, E)
+
+        def gather_late(a, lo, hi):
+            base = 0 if a == last else E - GROUP - 2
+            gather(late_words[:, (base + lo) * C : (base + hi) * C], codes[a], lo * C, hi * C)
+
         for q in range(4):
             nc.sync.dma_start(moved_first[32 * q : 32 * q + 4, :].bitcast(I32), got[SPARE + 4 * q : SPARE + 4 * q + 4, : JOINED * C].bitcast(I32))
         name_slots("first_bytes", moved_first, 0, JOINED)
-        gather(got[:, S - GROUP_SLOTS :], planes[:], S - GROUP_SLOTS, S)
-        nc.sync.dma_start(moved[:MOVED_ROWS, :].bitcast(I32), got[ROW[MOVED_PASS] : ROW[MOVED_PASS] + MOVED_ROWS, :].bitcast(I32))
-        for a in (fourth, last):
-            load_weights(a, E - GROUP, E)
+        for lo, hi in ((0, S - GROUP_SLOTS), (S - GROUP_SLOTS, S)):
+            nc.sync.dma_start(moved[:MOVED_ROWS, lo:hi].bitcast(I32), got[ROW[MOVED_PASS] : ROW[MOVED_PASS] + MOVED_ROWS, lo:hi].bitcast(I32))
+        for lo, hi in ((E - GROUP, E - 2), (E - 2, E)):
+            both_passes = keep.tile([P, (hi - lo) * FP8_PASSES, 4 * N], U8, name=f"both_passes{lo}", align_bytes=64)
+            nc.sync.dma_start(both_passes[:].bitcast(I32), w_views[FP8_PASSES][:, lo * FP8_PASSES : hi * FP8_PASSES, :].bitcast(I32))
+            for e in range(lo, hi):
+                for a in (fourth, last):
+                    weights[a, e] = both_passes[:, (e - lo) * FP8_PASSES + a, :]
         for tile, source in ((pos1_t, pos1), (pos2_t, pos2)):
             nc.sync.dma_start(tile[:], source)
 
@@ -268,22 +277,22 @@ def tile_moe_pln_lin_none_kernel(tc, xT, w8_words, w8_scales, w4_words, w4_scale
         multiply(fourth, group_a)
         multiply(second, group_b)
         multiply(second, group_c)
-        gather_late(GROUP + 2, E - GROUP)
+        gather_late(fourth, GROUP + 2, E - GROUP)
         multiply(fourth, group_b)
-        gather_group(f"words{last}", codes[last], U32, 0)
+        gather_late(last, 0, GROUP)
         multiply(last, group_a)
         multiply(first, range(JOINED))
-        gather_group(f"words{last}", codes[last], U32, 1)
+        gather_late(last, GROUP, 2 * GROUP)
         multiply(last, group_b)
-        gather_late(E - GROUP, E)
+        gather_late(fourth, E - GROUP, E)
         multiply(third, group_a, stop=True)
         empty_group(0)
         multiply(third, group_b, stop=True)
         empty_group(1)
         multiply(third, group_c)
-        multiply(fourth, group_c)
         for lo, hi in LAST_RUNS:
-            gather_run(f"words{last}", codes[last], U32, lo, hi)
+            gather_late(last, lo, hi)
+            multiply(fourth, range(lo, hi))
             multiply(last, range(lo, hi), stop=True)
             for e in range(lo, hi):
                 empty(e, on_vector=(e == E - 2))

@@ -29,15 +29,17 @@ FP8_SCALE_ROW = 8
 MOVED_PASS = 4
 MOVED_ROWS = 100
 LAST_QUADRANT = 96
-JOINED = 6
+JOINED = 8
 SPARE = 112
 
 HALF = 512
 HALVES = ((0, HALF), (HALF, T))
 WHOLE = ((0, T),)
-LOADS = (HALVES, HALVES, WHOLE, WHOLE, WHOLE)
+EVEN = ((0, T // 2), (T // 2, T))
+LOADS = (HALVES, EVEN, WHOLE, WHOLE, WHOLE)
 VECTOR_CASTS_TO = (320, 640)
 LAST_CAST = 16
+AHEAD = 6
 
 GROUP = 4
 GROUPS = E // GROUP
@@ -141,7 +143,9 @@ def tile_moe_pln_lin_none_kernel(tc, xT, w8_words, w8_scales, w4_words, w4_scale
             )
 
         def prepare(a):
-            for lo, hi in ((0, HALF - LAST_CAST), (HALF, T), (HALF - LAST_CAST, HALF)):
+            first_piece = LOADS[ORDER.index(a)][0][1]
+            cuts = ((0, first_piece), (first_piece, HALF - LAST_CAST)) if first_piece < HALF else ((0, HALF - LAST_CAST),)
+            for lo, hi in (*cuts, (HALF, T), (HALF - LAST_CAST, HALF)):
                 cast(a, lo, hi)
             for lo, hi in reversed(HALVES):
                 quantise(a, lo, hi)
@@ -160,9 +164,6 @@ def tile_moe_pln_lin_none_kernel(tc, xT, w8_words, w8_scales, w4_words, w4_scale
             tile = keep.tile([P, (hi - lo) * C], dtype, name=f"{what}_{lo}", tag=tag, align_bytes=64)
             gather(tile[:], window, lo * C, hi * C)
             name_slots(what, tile, lo, hi)
-
-        def gather_group(what, window, dtype, g, behind=None):
-            gather_run(what, window, dtype, g * GROUP, (g + 1) * GROUP, behind)
 
         for (lo, hi), mark in zip(HALVES, VECTOR_CASTS_TO):
             cast(first, lo, mark, on_vector=True)
@@ -189,9 +190,9 @@ def tile_moe_pln_lin_none_kernel(tc, xT, w8_words, w8_scales, w4_words, w4_scale
             gather_run(f"words{a}", wide[a], U32, 0, E - 1)
             prepare(following)
             gather_run(f"words{a}", codes[a], U32, E - 1, E, behind=following)
-        gather_group(f"words{fourth}", codes[fourth], U32, 0)
+        gather_run(f"words{fourth}", wide[fourth], U32, 0, AHEAD)
         prepare(last)
-        gather_run(f"words{fourth}", codes[fourth], U32, GROUP, GROUP + 1, behind=last)
+        gather_run(f"words{fourth}", codes[fourth], U32, AHEAD, AHEAD + 1, behind=last)
         turned = psum.tile([P, P], F32, name="turned", tag="shared0")
         nc.tensor.transpose(turned[:], gate_rows[:], identity[:])
         gate_columns = keep.tile([P, GATE_ROWS], F32, name="gate_columns", tag=f"raw{last}_0", align_bytes=64)
@@ -206,30 +207,30 @@ def tile_moe_pln_lin_none_kernel(tc, xT, w8_words, w8_scales, w4_words, w4_scale
         nc.vector.tensor_copy(joined[:SPARE, :].bitcast(I32), planes[:SPARE, :].bitcast(I32))
 
         between = keep.tile([P, C], U32, name="between", tag=f"grouped{last}_0", align_bytes=64)
-        gather(between[:], codes[fourth], (GROUP + 1) * C, (GROUP + 2) * C)
-        name_slots(f"words{fourth}", between, GROUP + 1, GROUP + 2)
+        gather(between[:], codes[fourth], (AHEAD + 1) * C, (AHEAD + 2) * C)
+        name_slots(f"words{fourth}", between, AHEAD + 1, AHEAD + 2)
         got = keep.tile([P, S], U8, name="got", align_bytes=64)
         for g in range(GROUPS):
             gather(got[:, g * GROUP_SLOTS : (g + 1) * GROUP_SLOTS], joined[:], g * GROUP_SLOTS, (g + 1) * GROUP_SLOTS)
-        late_words = keep.tile([P, (2 * E - GROUP - 2) * C], U32, name="late_words", tag="planes", align_bytes=64)
+        late_words = keep.tile([P, (2 * E - AHEAD - 2) * C], U32, name="late_words", tag="planes", align_bytes=64)
         name_slots(f"words{last}", late_words, 0, E)
-        name_slots(f"words{fourth}", late_words[:, S:], GROUP + 2, E)
+        name_slots(f"words{fourth}", late_words[:, S:], AHEAD + 2, E)
 
         def gather_late(a, lo, hi):
-            base = 0 if a == last else E - GROUP - 2
+            base = 0 if a == last else E - AHEAD - 2
             gather(late_words[:, (base + lo) * C : (base + hi) * C], codes[a], lo * C, hi * C)
 
         for q in range(4):
             nc.sync.dma_start(moved_first[32 * q : 32 * q + 4, :].bitcast(I32), got[SPARE + 4 * q : SPARE + 4 * q + 4, : JOINED * C].bitcast(I32))
         name_slots("first_bytes", moved_first, 0, JOINED)
-        for lo, hi in ((0, S - GROUP_SLOTS), (S - GROUP_SLOTS, S)):
+        for (lo, hi), experts in (((0, S - GROUP_SLOTS), range(E - GROUP, E - 2)), ((S - GROUP_SLOTS, S), range(E - 2, E))):
             nc.sync.dma_start(moved[:MOVED_ROWS, lo:hi].bitcast(I32), got[ROW[MOVED_PASS] : ROW[MOVED_PASS] + MOVED_ROWS, lo:hi].bitcast(I32))
-        for lo, hi in ((E - GROUP, E - 2), (E - 2, E)):
-            both_passes = keep.tile([P, (hi - lo) * FP8_PASSES, 4 * N], U8, name=f"both_passes{lo}", align_bytes=64)
-            nc.sync.dma_start(both_passes[:].bitcast(I32), w_views[FP8_PASSES][:, lo * FP8_PASSES : hi * FP8_PASSES, :].bitcast(I32))
-            for e in range(lo, hi):
+            rows = slice(experts.start * FP8_PASSES, experts.stop * FP8_PASSES)
+            both_passes = keep.tile([P, len(experts) * FP8_PASSES, 4 * N], U8, name=f"both_passes{experts.start}", align_bytes=64)
+            nc.sync.dma_start(both_passes[:].bitcast(I32), w_views[FP8_PASSES][:, rows, :].bitcast(I32))
+            for e in experts:
                 for a in (fourth, last):
-                    weights[a, e] = both_passes[:, (e - lo) * FP8_PASSES + a, :]
+                    weights[a, e] = both_passes[:, e * FP8_PASSES + a - rows.start, :]
         for tile, source in ((pos1_t, pos1), (pos2_t, pos2)):
             nc.sync.dma_start(tile[:], source)
 
@@ -238,10 +239,13 @@ def tile_moe_pln_lin_none_kernel(tc, xT, w8_words, w8_scales, w4_words, w4_scale
         sums = {e: shared[e // GROUP][:, e % GROUP * C : (e % GROUP + 1) * C] for e in range(E - GROUP)}
         sums.update({e: psum.tile([N, C], F32, name=f"sum{e}")[:] for e in range(E - GROUP, E)})
 
-        def multiply(a, experts, start=False, stop=False):
+        done = {}
+
+        def multiply(a, experts):
             for e in experts:
-                g, m = divmod(e, GROUP)
-                alone = g == GROUPS - 1
+                alone = e >= E - GROUP
+                bank = e if alone else e // GROUP
+                done[bank] = done.get(bank, 0) + 1
                 if a < FP8_PASSES:
                     lhsT = weights[a, e].bitcast(FP8X4)
                     lhsT_scale = w8s[FP8_SCALE_ROW:P, e * FP8_PASSES + a, :]
@@ -257,7 +261,7 @@ def tile_moe_pln_lin_none_kernel(tc, xT, w8_words, w8_scales, w4_words, w4_scale
                 nc.tensor.matmul_mx(
                     out=sums[e], lhsT=lhsT, lhsT_scale=lhsT_scale,
                     rhs=slots[f"words{a}", e].bitcast(FP8X4), rhs_scale=rhs_scale,
-                    start=start and (alone or e == experts.start), stop=stop and (alone or m == GROUP - 1),
+                    start=done[bank] == 1, stop=done[bank] == PASSES * (1 if alone else GROUP),
                 )
 
         def empty(e, on_vector=False):
@@ -271,13 +275,11 @@ def tile_moe_pln_lin_none_kernel(tc, xT, w8_words, w8_scales, w4_words, w4_scale
             nc.scalar.copy(y[:, g * GROUP_SLOTS : (g + 1) * GROUP_SLOTS], shared[g][:])
 
         group_a, group_b, group_c = (range(g * GROUP, (g + 1) * GROUP) for g in range(GROUPS))
-        multiply(first, group_c, start=True)
-        multiply(first, range(JOINED, E - GROUP), start=True)
-        multiply(second, group_a, start=True)
+        multiply(first, range(JOINED, E))
+        multiply(second, group_a)
         multiply(fourth, group_a)
         multiply(second, group_b)
         multiply(second, group_c)
-        gather_late(fourth, GROUP + 2, E - GROUP)
         multiply(fourth, group_b)
         gather_late(last, 0, GROUP)
         multiply(last, group_a)
@@ -285,15 +287,15 @@ def tile_moe_pln_lin_none_kernel(tc, xT, w8_words, w8_scales, w4_words, w4_scale
         gather_late(last, GROUP, 2 * GROUP)
         multiply(last, group_b)
         gather_late(fourth, E - GROUP, E)
-        multiply(third, group_a, stop=True)
+        multiply(third, group_a)
         empty_group(0)
-        multiply(third, group_b, stop=True)
+        multiply(third, group_b)
         empty_group(1)
         multiply(third, group_c)
         for lo, hi in LAST_RUNS:
             gather_late(last, lo, hi)
             multiply(fourth, range(lo, hi))
-            multiply(last, range(lo, hi), stop=True)
+            multiply(last, range(lo, hi))
             for e in range(lo, hi):
                 empty(e, on_vector=(e == E - 2))
 

@@ -39,6 +39,8 @@ EVEN = ((0, T // 2), (T // 2, T))
 LOADS = (HALVES, EVEN, WHOLE, WHOLE, WHOLE)
 VECTOR_CASTS_TO = (320, 640)
 LAST_CAST = 16
+THIRDS = ((0, HALF), (HALF, 640), (640, T))
+PIECES = dict(zip(ORDER, (HALVES, HALVES, THIRDS, HALVES, THIRDS)))
 AHEAD = 6
 
 GROUP = 4
@@ -117,14 +119,14 @@ def tile_moe_pln_lin_none_kernel(tc, xT, w8_words, w8_scales, w4_words, w4_scale
         grouped = {
             (a, lo): keep.tile([P, hi - lo, 4], BF16, name=f"grouped{a}_{lo}", tag=f"grouped{a}_{lo}", align_bytes=64)
             for a in ORDER
-            for lo, hi in HALVES
+            for lo, hi in PIECES[a]
         }
         base_of = {a: (PASSES - 1 - i) * T for i, a in enumerate(ORDER)}
         codes = {a: all_codes[:, base_of[a] : base_of[a] + T] for a in ORDER}
         wide = {a: all_codes[:, base_of[a] : base_of[a] + WIDE] for a in ORDER}
 
         def cast(a, lo, hi, on_vector=False):
-            piece = 0 if hi <= HALF else HALF
+            piece = max(start for start, end in PIECES[a] if start <= lo)
             dst = grouped[a, piece][:, lo - piece : hi - piece, :].rearrange("p (c i) j -> p c j i", i=4)
             for base, end, part in raw[a]:
                 if base <= lo and hi <= end:
@@ -143,12 +145,16 @@ def tile_moe_pln_lin_none_kernel(tc, xT, w8_words, w8_scales, w4_words, w4_scale
             )
 
         def prepare(a):
-            first_piece = LOADS[ORDER.index(a)][0][1]
-            cuts = ((0, first_piece), (first_piece, HALF - LAST_CAST)) if first_piece < HALF else ((0, HALF - LAST_CAST),)
-            for lo, hi in (*cuts, (HALF, T), (HALF - LAST_CAST, HALF)):
-                cast(a, lo, hi)
-            for lo, hi in reversed(HALVES):
-                quantise(a, lo, hi)
+            *lead, (lo, hi), final = PIECES[a]
+            for piece in lead:
+                cast(a, *piece)
+                quantise(a, *piece)
+            landed = LOADS[ORDER.index(a)][0][1]
+            cuts = ((lo, landed), (landed, hi - LAST_CAST)) if lo < landed < hi else ((lo, hi - LAST_CAST),)
+            for piece in (*cuts, final, (hi - LAST_CAST, hi)):
+                cast(a, *piece)
+            for piece in (final, (lo, hi)):
+                quantise(a, *piece)
 
         def gather(dst, window, lo, hi):
             nc.vector.tensor_copy(dst, window.indirect(offs_t[:, lo // 16 : hi // 16]))
@@ -160,7 +166,7 @@ def tile_moe_pln_lin_none_kernel(tc, xT, w8_words, w8_scales, w4_words, w4_scale
                 slots[what, e] = tile[:, (e - lo) * C : (e - lo + 1) * C]
 
         def gather_run(what, window, dtype, lo, hi, behind=None):
-            tag = f"{what}_{lo}" if behind is None else f"grouped{behind}_{HALF}"
+            tag = f"{what}_{lo}" if behind is None else f"grouped{behind}_{PIECES[behind][-1][0]}"
             tile = keep.tile([P, (hi - lo) * C], dtype, name=f"{what}_{lo}", tag=tag, align_bytes=64)
             gather(tile[:], window, lo * C, hi * C)
             name_slots(what, tile, lo, hi)
@@ -206,7 +212,7 @@ def tile_moe_pln_lin_none_kernel(tc, xT, w8_words, w8_scales, w4_words, w4_scale
             nc.scalar.copy(gate_t[:].rearrange("p c t -> p (c t)")[:, b * GROUP * P : (b + 1) * GROUP * P], bank[:].rearrange("p m n -> p (m n)"))
         nc.vector.tensor_copy(joined[:SPARE, :].bitcast(I32), planes[:SPARE, :].bitcast(I32))
 
-        between = keep.tile([P, C], U32, name="between", tag=f"grouped{last}_0", align_bytes=64)
+        between = keep.tile([P, C], U32, name="between", tag=f"grouped{last}_{HALF}", align_bytes=64)
         gather(between[:], codes[fourth], (AHEAD + 1) * C, (AHEAD + 2) * C)
         name_slots(f"words{fourth}", between, AHEAD + 1, AHEAD + 2)
         got = keep.tile([P, S], U8, name="got", align_bytes=64)

@@ -29,7 +29,7 @@ FP8_SCALE_ROW = 8
 MOVED_PASS = 4
 MOVED_ROWS = 100
 LAST_QUADRANT = 96
-JOINED = 8
+JOINED = 10
 SPARE = 112
 
 HALF = 512
@@ -40,7 +40,7 @@ LOADS = (HALVES, EVEN, WHOLE, WHOLE, WHOLE)
 VECTOR_CASTS_TO = (320, 640)
 LAST_CAST = 16
 THIRDS = ((0, HALF), (HALF, 640), (640, T))
-PIECES = dict(zip(ORDER, (HALVES, HALVES, THIRDS, HALVES, THIRDS)))
+PIECES = dict(zip(ORDER, (HALVES, THIRDS, THIRDS, HALVES, THIRDS)))
 AHEAD = 6
 
 GROUP = 4
@@ -49,6 +49,7 @@ GROUP_SLOTS = GROUP * C
 WIDE = 2048
 WIDE_BYTES = 1024
 GATE_ROWS = 2 * T // P
+SPREAD_BANKS = ("spread0", "spread1", "spread2")
 LAST_RUNS = ((8, 10), (10, 11), (11, 12))
 OUT_PIECES = ((0, 256, True), (256, 448, False), (448, 640, True), (640, T, True))
 
@@ -68,8 +69,8 @@ def tile_moe_pln_lin_none_kernel(tc, xT, w8_words, w8_scales, w4_words, w4_scale
         planes = keep.tile([P, T], U8, name="planes", tag="planes", align_bytes=64)
         moved = keep.tile([P, S], U8, name="moved", align_bytes=64)
         moved_first = keep.tile([P, JOINED * C], U8, name="moved_first", align_bytes=64)
-        joined = keep.tile([P, T], U8, name="joined", align_bytes=64)
-        for t in (first_plane[:], planes[:], moved_first[:]):
+        joined = keep.tile([P, WIDE_BYTES], U8, name="joined", align_bytes=64)
+        for t in (first_plane[:], planes[:], moved_first[:], joined[:, T:]):
             nc.vector.memset(t.bitcast(I32), 0)
         all_codes = keep.tile([P, (PASSES - 1) * T + WIDE], U32, name="all_codes", align_bytes=64)
         nc.vector.memset(all_codes[:, PASSES * T :].bitcast(I32), 0)
@@ -127,10 +128,11 @@ def tile_moe_pln_lin_none_kernel(tc, xT, w8_words, w8_scales, w4_words, w4_scale
 
         def cast(a, lo, hi, on_vector=False):
             piece = max(start for start, end in PIECES[a] if start <= lo)
-            dst = grouped[a, piece][:, lo - piece : hi - piece, :].rearrange("p (c i) j -> p c j i", i=4)
             for base, end, part in raw[a]:
-                if base <= lo and hi <= end:
-                    src = part[:, :, lo - base : hi - base].rearrange("p j (c i) -> p c j i", i=4)
+                start, stop = max(lo, base), min(hi, end)
+                if start < stop:
+                    dst = grouped[a, piece][:, start - piece : stop - piece, :].rearrange("p (c i) j -> p c j i", i=4)
+                    src = part[:, :, start - base : stop - base].rearrange("p j (c i) -> p c j i", i=4)
                     if on_vector:
                         nc.vector.tensor_copy(dst, src)
                     else:
@@ -149,9 +151,7 @@ def tile_moe_pln_lin_none_kernel(tc, xT, w8_words, w8_scales, w4_words, w4_scale
             for piece in lead:
                 cast(a, *piece)
                 quantise(a, *piece)
-            landed = LOADS[ORDER.index(a)][0][1]
-            cuts = ((lo, landed), (landed, hi - LAST_CAST)) if lo < landed < hi else ((lo, hi - LAST_CAST),)
-            for piece in (*cuts, final, (hi - LAST_CAST, hi)):
+            for piece in ((lo, hi - LAST_CAST), final, (hi - LAST_CAST, hi)):
                 cast(a, *piece)
             for piece in (final, (lo, hi)):
                 quantise(a, *piece)
@@ -177,7 +177,7 @@ def tile_moe_pln_lin_none_kernel(tc, xT, w8_words, w8_scales, w4_words, w4_scale
             quantise(first, lo, hi)
         gather_run(f"words{first}", wide[first], U32, 0, E)
         for q in range(4):
-            nc.sync.dma_start(joined[SPARE + 4 * q : SPARE + 4 * q + 4, :].bitcast(I32), first_plane[32 * q : 32 * q + 4, :T].bitcast(I32))
+            nc.sync.dma_start(joined[SPARE + 4 * q : SPARE + 4 * q + 4, :T].bitcast(I32), first_plane[32 * q : 32 * q + 4, :T].bitcast(I32))
         load_pass(fourth)
         load_pass(last)
         w4s = keep.tile([P, E * FP4_PASSES, N], U8, name="w4s", tag=f"raw{first}_0", align_bytes=64)
@@ -199,25 +199,25 @@ def tile_moe_pln_lin_none_kernel(tc, xT, w8_words, w8_scales, w4_words, w4_scale
         gather_run(f"words{fourth}", wide[fourth], U32, 0, AHEAD)
         prepare(last)
         gather_run(f"words{fourth}", codes[fourth], U32, AHEAD, AHEAD + 1, behind=last)
-        turned = psum.tile([P, P], F32, name="turned", tag="shared0")
+        turned = psum.tile([P, P], F32, name="turned", tag="turned")
         nc.tensor.transpose(turned[:], gate_rows[:], identity[:])
         gate_columns = keep.tile([P, GATE_ROWS], F32, name="gate_columns", tag=f"raw{last}_0", align_bytes=64)
         nc.scalar.copy(gate_columns[:], turned[:, :GATE_ROWS])
         gate_t = keep.tile([P, 2, T], F32, name="gate_t")
-        for b, tag in enumerate(("spread0", "spread1", "shared1")):
+        for b, tag in enumerate(SPREAD_BANKS):
             bank = psum.tile([P, GROUP, P], F32, name=f"spread{b}", tag=tag)
             for m in range(GROUP):
                 column = gate_columns[:, GROUP * b + m : GROUP * b + m + 1]
                 nc.tensor.transpose(bank[:, m, :], column.to_broadcast([P, P]), identity[:])
             nc.scalar.copy(gate_t[:].rearrange("p c t -> p (c t)")[:, b * GROUP * P : (b + 1) * GROUP * P], bank[:].rearrange("p m n -> p (m n)"))
-        nc.vector.tensor_copy(joined[:SPARE, :].bitcast(I32), planes[:SPARE, :].bitcast(I32))
+        nc.vector.tensor_copy(joined[:SPARE, :T].bitcast(I32), planes[:SPARE, :].bitcast(I32))
 
         between = keep.tile([P, C], U32, name="between", tag=f"grouped{last}_{HALF}", align_bytes=64)
         gather(between[:], codes[fourth], (AHEAD + 1) * C, (AHEAD + 2) * C)
         name_slots(f"words{fourth}", between, AHEAD + 1, AHEAD + 2)
         got = keep.tile([P, S], U8, name="got", align_bytes=64)
-        for g in range(GROUPS):
-            gather(got[:, g * GROUP_SLOTS : (g + 1) * GROUP_SLOTS], joined[:], g * GROUP_SLOTS, (g + 1) * GROUP_SLOTS)
+        for lo, hi in ((0, JOINED * C // 2), (JOINED * C // 2, JOINED * C), (JOINED * C, S)):
+            gather(got[:, lo:hi], joined[:], lo, hi)
         late_words = keep.tile([P, (2 * E - AHEAD - 2) * C], U32, name="late_words", tag="planes", align_bytes=64)
         name_slots(f"words{last}", late_words, 0, E)
         name_slots(f"words{fourth}", late_words[:, S:], AHEAD + 2, E)
@@ -229,7 +229,7 @@ def tile_moe_pln_lin_none_kernel(tc, xT, w8_words, w8_scales, w4_words, w4_scale
         for q in range(4):
             nc.sync.dma_start(moved_first[32 * q : 32 * q + 4, :].bitcast(I32), got[SPARE + 4 * q : SPARE + 4 * q + 4, : JOINED * C].bitcast(I32))
         name_slots("first_bytes", moved_first, 0, JOINED)
-        for (lo, hi), experts in (((0, S - GROUP_SLOTS), range(E - GROUP, E - 2)), ((S - GROUP_SLOTS, S), range(E - 2, E))):
+        for (lo, hi), experts in (((0, JOINED * C), range(E - GROUP, E - 2)), ((JOINED * C, S), range(E - 2, E))):
             nc.sync.dma_start(moved[:MOVED_ROWS, lo:hi].bitcast(I32), got[ROW[MOVED_PASS] : ROW[MOVED_PASS] + MOVED_ROWS, lo:hi].bitcast(I32))
             rows = slice(experts.start * FP8_PASSES, experts.stop * FP8_PASSES)
             both_passes = keep.tile([P, len(experts) * FP8_PASSES, 4 * N], U8, name=f"both_passes{experts.start}", align_bytes=64)
@@ -241,8 +241,8 @@ def tile_moe_pln_lin_none_kernel(tc, xT, w8_words, w8_scales, w4_words, w4_scale
             nc.sync.dma_start(tile[:], source)
 
         y = keep.tile([P, S], F32, name="y")
-        shared = [psum.tile([N, GROUP_SLOTS], F32, name=f"shared{g}", tag=f"shared{g}") for g in range(GROUPS - 1)]
-        sums = {e: shared[e // GROUP][:, e % GROUP * C : (e % GROUP + 1) * C] for e in range(E - GROUP)}
+        pairs = [psum.tile([N, 2 * C], F32, name=f"pair{b}", tag=tag) for b, tag in enumerate(("turned", *SPREAD_BANKS))]
+        sums = {e: pairs[e // 2][:, e % 2 * C : (e % 2 + 1) * C] for e in range(E - GROUP)}
         sums.update({e: psum.tile([N, C], F32, name=f"sum{e}")[:] for e in range(E - GROUP, E)})
 
         done = {}
@@ -250,7 +250,7 @@ def tile_moe_pln_lin_none_kernel(tc, xT, w8_words, w8_scales, w4_words, w4_scale
         def multiply(a, experts):
             for e in experts:
                 alone = e >= E - GROUP
-                bank = e if alone else e // GROUP
+                bank = e if alone else e // 2
                 done[bank] = done.get(bank, 0) + 1
                 if a < FP8_PASSES:
                     lhsT = weights[a, e].bitcast(FP8X4)
@@ -267,7 +267,7 @@ def tile_moe_pln_lin_none_kernel(tc, xT, w8_words, w8_scales, w4_words, w4_scale
                 nc.tensor.matmul_mx(
                     out=sums[e], lhsT=lhsT, lhsT_scale=lhsT_scale,
                     rhs=slots[f"words{a}", e].bitcast(FP8X4), rhs_scale=rhs_scale,
-                    start=done[bank] == 1, stop=done[bank] == PASSES * (1 if alone else GROUP),
+                    start=done[bank] == 1, stop=done[bank] == PASSES * (1 if alone else 2),
                 )
 
         def empty(e, on_vector=False):
@@ -277,8 +277,8 @@ def tile_moe_pln_lin_none_kernel(tc, xT, w8_words, w8_scales, w4_words, w4_scale
             else:
                 nc.scalar.copy(dst, sums[e])
 
-        def empty_group(g):
-            nc.scalar.copy(y[:, g * GROUP_SLOTS : (g + 1) * GROUP_SLOTS], shared[g][:])
+        def empty_pair(b):
+            nc.scalar.copy(y[:, 2 * b * C : 2 * (b + 1) * C], pairs[b][:])
 
         group_a, group_b, group_c = (range(g * GROUP, (g + 1) * GROUP) for g in range(GROUPS))
         multiply(first, range(JOINED, E))
@@ -292,11 +292,10 @@ def tile_moe_pln_lin_none_kernel(tc, xT, w8_words, w8_scales, w4_words, w4_scale
         multiply(first, range(JOINED))
         gather_late(last, GROUP, 2 * GROUP)
         multiply(last, group_b)
-        gather_late(fourth, E - GROUP, E)
-        multiply(third, group_a)
-        empty_group(0)
-        multiply(third, group_b)
-        empty_group(1)
+        gather_late(fourth, AHEAD + 2, E)
+        for b in range(len(pairs)):
+            multiply(third, range(2 * b, 2 * b + 2))
+            empty_pair(b)
         multiply(third, group_c)
         for lo, hi in LAST_RUNS:
             gather_late(last, lo, hi)

@@ -112,6 +112,13 @@ def tile_moe_pln_lin_none_kernel(tc, xT, w8_words, w8_scales, w4_words, w4_scale
             for e in range(lo, hi):
                 weights[a, e] = tile[:, e - lo, :]
 
+        def load_both_passes(lo, hi):
+            tile = keep.tile([P, (hi - lo) * FP8_PASSES, 4 * N], U8, name=f"both_passes{lo}", align_bytes=64)
+            nc.sync.dma_start(tile[:].bitcast(I32), w_views[FP8_PASSES][:, lo * FP8_PASSES : hi * FP8_PASSES, :].bitcast(I32))
+            for e in range(lo, hi):
+                for a in (fourth, last):
+                    weights[a, e] = tile[:, (e - lo) * FP8_PASSES + a, :]
+
         def load_scales(rows):
             for r in rows:
                 for scales, source, row in ((w4s, w4_scales, 0), (w8s, w8_scales, FP8_SCALE_ROW)):
@@ -189,6 +196,7 @@ def tile_moe_pln_lin_none_kernel(tc, xT, w8_words, w8_scales, w4_words, w4_scale
         load_weights(fourth, 0, E - GROUP)
         load_weights(last, 0, E - GROUP)
         load_weights(third, 0, E)
+        load_both_passes(E - GROUP, E - 2)
         gather_run("first_bytes", first_plane[:], U8, JOINED, E - 1)
         prepare(second)
         gather_run("first_bytes", first_plane[:], U8, E - 1, E, behind=second)
@@ -226,17 +234,15 @@ def tile_moe_pln_lin_none_kernel(tc, xT, w8_words, w8_scales, w4_words, w4_scale
             base = 0 if a == last else E - AHEAD - 2
             gather(late_words[:, (base + lo) * C : (base + hi) * C], codes[a], lo * C, hi * C)
 
+        def move_up(lo, hi):
+            nc.sync.dma_start(moved[:MOVED_ROWS, lo:hi].bitcast(I32), got[ROW[MOVED_PASS] : ROW[MOVED_PASS] + MOVED_ROWS, lo:hi].bitcast(I32))
+
         for q in range(4):
             nc.sync.dma_start(moved_first[32 * q : 32 * q + 4, :].bitcast(I32), got[SPARE + 4 * q : SPARE + 4 * q + 4, : JOINED * C].bitcast(I32))
         name_slots("first_bytes", moved_first, 0, JOINED)
-        for (lo, hi), experts in (((0, JOINED * C), range(E - GROUP, E - 2)), ((JOINED * C, S), range(E - 2, E))):
-            nc.sync.dma_start(moved[:MOVED_ROWS, lo:hi].bitcast(I32), got[ROW[MOVED_PASS] : ROW[MOVED_PASS] + MOVED_ROWS, lo:hi].bitcast(I32))
-            rows = slice(experts.start * FP8_PASSES, experts.stop * FP8_PASSES)
-            both_passes = keep.tile([P, len(experts) * FP8_PASSES, 4 * N], U8, name=f"both_passes{experts.start}", align_bytes=64)
-            nc.sync.dma_start(both_passes[:].bitcast(I32), w_views[FP8_PASSES][:, rows, :].bitcast(I32))
-            for e in experts:
-                for a in (fourth, last):
-                    weights[a, e] = both_passes[:, e * FP8_PASSES + a - rows.start, :]
+        move_up(0, JOINED * C)
+        load_both_passes(E - 2, E)
+        move_up(JOINED * C, S)
         for tile, source in ((pos1_t, pos1), (pos2_t, pos2)):
             nc.sync.dma_start(tile[:], source)
 
@@ -296,11 +302,10 @@ def tile_moe_pln_lin_none_kernel(tc, xT, w8_words, w8_scales, w4_words, w4_scale
         for b in range(len(pairs)):
             multiply(third, range(2 * b, 2 * b + 2))
             empty_pair(b)
-        multiply(third, group_c)
         for lo, hi in LAST_RUNS:
             gather_late(last, lo, hi)
-            multiply(fourth, range(lo, hi))
-            multiply(last, range(lo, hi))
+            for a in (third, fourth, last):
+                multiply(a, range(lo, hi))
             for e in range(lo, hi):
                 empty(e, on_vector=(e == E - 2))
 

@@ -22,6 +22,7 @@ PASSES = K // 512
 FP8_PASSES = 2
 FP4_PASSES = PASSES - FP8_PASSES
 FLOPS = 2 * K * N * S
+LINE = 256
 
 ORDER = (2, 3, 4, 0, 1)
 ROW = {2: 0, 3: 0, 4: 12, 0: 4, 1: 8}
@@ -61,18 +62,18 @@ def tile_moe_pln_lin_none_kernel(tc, xT, w8_words, w8_scales, w4_words, w4_scale
         keep = ctx.enter_context(tc.tile_pool(name="keep", bufs=1))
         psum = ctx.enter_context(tc.psum_pool(name="psum", bufs=1))
 
-        offs_t = keep.tile([P, S // 16], U16, name="offs_t")
-        pos1_t = keep.tile([P, T // 16], U16, name="pos1_t")
-        pos2_t = keep.tile([P, T // 16], U16, name="pos2_t")
+        offs_t = keep.tile([P, S // 16], U16, name="offs_t", align_bytes=LINE)
+        pos1_t = keep.tile([P, T // 16], U16, name="pos1_t", align_bytes=LINE)
+        pos2_t = keep.tile([P, T // 16], U16, name="pos2_t", align_bytes=LINE)
 
-        first_plane = keep.tile([P, WIDE_BYTES], U8, name="first_plane", align_bytes=64)
-        planes = keep.tile([P, T], U8, name="planes", tag="planes", align_bytes=64)
-        moved = keep.tile([P, S], U8, name="moved", align_bytes=64)
-        moved_first = keep.tile([P, JOINED * C], U8, name="moved_first", align_bytes=64)
-        joined = keep.tile([P, WIDE_BYTES], U8, name="joined", align_bytes=64)
+        first_plane = keep.tile([P, WIDE_BYTES], U8, name="first_plane", align_bytes=LINE)
+        planes = keep.tile([P, T], U8, name="planes", tag="planes", align_bytes=LINE)
+        moved = keep.tile([P, S], U8, name="moved", align_bytes=LINE)
+        moved_first = keep.tile([P, JOINED * C], U8, name="moved_first", align_bytes=LINE)
+        joined = keep.tile([P, WIDE_BYTES], U8, name="joined", align_bytes=LINE)
         for t in (first_plane[:], planes[:], moved_first[:], joined[:, T:]):
             nc.vector.memset(t.bitcast(I32), 0)
-        all_codes = keep.tile([P, (PASSES - 1) * T + WIDE], U32, name="all_codes", align_bytes=64)
+        all_codes = keep.tile([P, (PASSES - 1) * T + WIDE], U32, name="all_codes", align_bytes=LINE)
         nc.vector.memset(all_codes[:, PASSES * T :].bitcast(I32), 0)
         nc.vector.memset(moved[LAST_QUADRANT:P, :].bitcast(I32), 0)
 
@@ -82,7 +83,7 @@ def tile_moe_pln_lin_none_kernel(tc, xT, w8_words, w8_scales, w4_words, w4_scale
         def load_pass(a):
             raw[a] = []
             for lo, hi in LOADS[ORDER.index(a)]:
-                part = keep.tile([P, 4, hi - lo], F32, name=f"raw{a}_{lo}", tag=f"raw{a}_{lo}", align_bytes=64)
+                part = keep.tile([P, 4, hi - lo], F32, name=f"raw{a}_{lo}", tag=f"raw{a}_{lo}", align_bytes=LINE)
                 nc.sync.dma_start(part[:], x_view[a][:, :, lo:hi])
                 raw[a].append((lo, hi, part))
 
@@ -93,7 +94,7 @@ def tile_moe_pln_lin_none_kernel(tc, xT, w8_words, w8_scales, w4_words, w4_scale
 
         identity = keep.tile([P, P], F32, name="identity")
         make_identity(nc, identity[:])
-        gate_rows = keep.tile([P, P], F32, name="gate_rows")
+        gate_rows = keep.tile([P, P], F32, name="gate_rows", align_bytes=LINE)
         nc.gpsimd.memset(gate_rows[:], 0.0)
         both = gate.rearrange("c r (m n) -> (c r m) n", n=P)
         nc.sync.dma_start(gate_rows[:GATE_ROWS, :], both[(N - 1) * T // P : (N + 1) * T // P, :])
@@ -107,13 +108,13 @@ def tile_moe_pln_lin_none_kernel(tc, xT, w8_words, w8_scales, w4_words, w4_scale
 
         def load_weights(a, lo, hi):
             passes, index, width = (FP8_PASSES, a, 4 * N) if a < FP8_PASSES else (FP4_PASSES, a - FP8_PASSES, 2 * N)
-            tile = keep.tile([P, hi - lo, width], U8, name=f"weights{a}_{lo}", align_bytes=64)
+            tile = keep.tile([P, hi - lo, width], U8, name=f"weights{a}_{lo}", align_bytes=LINE)
             nc.sync.dma_start(tile[:].bitcast(I32), w_views[passes][:, lo * passes + index : hi * passes : passes, :].bitcast(I32))
             for e in range(lo, hi):
                 weights[a, e] = tile[:, e - lo, :]
 
         def load_both_passes(lo, hi):
-            tile = keep.tile([P, (hi - lo) * FP8_PASSES, 4 * N], U8, name=f"both_passes{lo}", align_bytes=64)
+            tile = keep.tile([P, (hi - lo) * FP8_PASSES, 4 * N], U8, name=f"both_passes{lo}", align_bytes=LINE)
             nc.sync.dma_start(tile[:].bitcast(I32), w_views[FP8_PASSES][:, lo * FP8_PASSES : hi * FP8_PASSES, :].bitcast(I32))
             for e in range(lo, hi):
                 for a in (fourth, last):
@@ -122,10 +123,10 @@ def tile_moe_pln_lin_none_kernel(tc, xT, w8_words, w8_scales, w4_words, w4_scale
         def load_scales(rows):
             for r in rows:
                 for scales, source, row in ((w4s, w4_scales, 0), (w8s, w8_scales, FP8_SCALE_ROW)):
-                    nc.sync.dma_start(scales[row + r : P : 32].bitcast(I32), source[:, :, r:16:4, :].rearrange("e a q n -> q (e a) n").bitcast(I32))
+                    nc.sync.dma_start(scales[row + r : P : 32, :, :N].bitcast(I32), source[:, :, r:16:4, :].rearrange("e a q n -> q (e a) n").bitcast(I32))
 
         grouped = {
-            (a, lo): keep.tile([P, hi - lo, 4], BF16, name=f"grouped{a}_{lo}", tag=f"grouped{a}_{lo}", align_bytes=64)
+            (a, lo): keep.tile([P, hi - lo, 4], BF16, name=f"grouped{a}_{lo}", tag=f"grouped{a}_{lo}", align_bytes=LINE)
             for a in ORDER
             for lo, hi in PIECES[a]
         }
@@ -174,7 +175,7 @@ def tile_moe_pln_lin_none_kernel(tc, xT, w8_words, w8_scales, w4_words, w4_scale
 
         def gather_run(what, window, dtype, lo, hi, behind=None):
             tag = f"{what}_{lo}" if behind is None else f"grouped{behind}_{PIECES[behind][-1][0]}"
-            tile = keep.tile([P, (hi - lo) * C], dtype, name=f"{what}_{lo}", tag=tag, align_bytes=64)
+            tile = keep.tile([P, (hi - lo) * C], dtype, name=f"{what}_{lo}", tag=tag, align_bytes=LINE)
             gather(tile[:], window, lo * C, hi * C)
             name_slots(what, tile, lo, hi)
 
@@ -187,8 +188,8 @@ def tile_moe_pln_lin_none_kernel(tc, xT, w8_words, w8_scales, w4_words, w4_scale
             nc.sync.dma_start(joined[SPARE + 4 * q : SPARE + 4 * q + 4, :T].bitcast(I32), first_plane[32 * q : 32 * q + 4, :T].bitcast(I32))
         load_pass(fourth)
         load_pass(last)
-        w4s = keep.tile([P, E * FP4_PASSES, N], U8, name="w4s", tag=f"raw{first}_0", align_bytes=64)
-        w8s = keep.tile([P, E * FP8_PASSES, N], U8, name="w8s", tag=f"raw{first}_{HALF}", align_bytes=64)
+        w4s = keep.tile([P, E * FP4_PASSES, LINE], U8, name="w4s", tag=f"raw{third}_0", align_bytes=LINE)
+        w8s = keep.tile([P, E * FP8_PASSES, LINE], U8, name="w8s", tag=f"raw{second}_0", align_bytes=LINE)
         load_weights(first, 0, E)
         load_scales((0, 1))
         load_weights(second, 0, E)
@@ -209,7 +210,7 @@ def tile_moe_pln_lin_none_kernel(tc, xT, w8_words, w8_scales, w4_words, w4_scale
         gather_run(f"words{fourth}", codes[fourth], U32, AHEAD, AHEAD + 1, behind=last)
         turned = psum.tile([P, P], F32, name="turned", tag="turned")
         nc.tensor.transpose(turned[:], gate_rows[:], identity[:])
-        gate_columns = keep.tile([P, GATE_ROWS], F32, name="gate_columns", tag=f"raw{last}_0", align_bytes=64)
+        gate_columns = keep.tile([P, GATE_ROWS], F32, name="gate_columns", tag=f"raw{last}_0", align_bytes=LINE)
         nc.scalar.copy(gate_columns[:], turned[:, :GATE_ROWS])
         gate_t = keep.tile([P, 2, T], F32, name="gate_t")
         for b, tag in enumerate(SPREAD_BANKS):
@@ -220,13 +221,13 @@ def tile_moe_pln_lin_none_kernel(tc, xT, w8_words, w8_scales, w4_words, w4_scale
             nc.scalar.copy(gate_t[:].rearrange("p c t -> p (c t)")[:, b * GROUP * P : (b + 1) * GROUP * P], bank[:].rearrange("p m n -> p (m n)"))
         nc.vector.tensor_copy(joined[:SPARE, :T].bitcast(I32), planes[:SPARE, :].bitcast(I32))
 
-        between = keep.tile([P, C], U32, name="between", tag=f"grouped{last}_{HALF}", align_bytes=64)
+        between = keep.tile([P, C], U32, name="between", tag=f"grouped{last}_{HALF}", align_bytes=LINE)
         gather(between[:], codes[fourth], (AHEAD + 1) * C, (AHEAD + 2) * C)
         name_slots(f"words{fourth}", between, AHEAD + 1, AHEAD + 2)
-        got = keep.tile([P, S], U8, name="got", align_bytes=64)
+        got = keep.tile([P, S], U8, name="got", align_bytes=LINE)
         for lo, hi in ((0, JOINED * C // 2), (JOINED * C // 2, JOINED * C), (JOINED * C, S)):
             gather(got[:, lo:hi], joined[:], lo, hi)
-        late_words = keep.tile([P, (2 * E - AHEAD - 2) * C], U32, name="late_words", tag="planes", align_bytes=64)
+        late_words = keep.tile([P, (2 * E - AHEAD - 2) * C], U32, name="late_words", tag="planes", align_bytes=LINE)
         name_slots(f"words{last}", late_words, 0, E)
         name_slots(f"words{fourth}", late_words[:, S:], AHEAD + 2, E)
 
@@ -260,10 +261,10 @@ def tile_moe_pln_lin_none_kernel(tc, xT, w8_words, w8_scales, w4_words, w4_scale
                 done[bank] = done.get(bank, 0) + 1
                 if a < FP8_PASSES:
                     lhsT = weights[a, e].bitcast(FP8X4)
-                    lhsT_scale = w8s[FP8_SCALE_ROW:P, e * FP8_PASSES + a, :]
+                    lhsT_scale = w8s[FP8_SCALE_ROW:P, e * FP8_PASSES + a, :N]
                 else:
                     lhsT = weights[a, e].bitcast(FP4X4)
-                    lhsT_scale = w4s[:, e * FP4_PASSES + a - FP8_PASSES, :]
+                    lhsT_scale = w4s[:, e * FP4_PASSES + a - FP8_PASSES, :N]
                 if a == first:
                     rhs_scale = slots["first_bytes", e]
                 elif a == MOVED_PASS:
@@ -325,7 +326,7 @@ def tile_moe_pln_lin_none_kernel(tc, xT, w8_words, w8_scales, w4_words, w4_scale
             nc.vector.tensor_tensor(products[lo][:, choices, :], fetched[lo][:], gate_t[:, choices, lo:hi], MULT)
 
         def finish(lo, hi, fused):
-            total = keep.tile([P, hi - lo], F32, name=f"total{lo}")
+            total = keep.tile([P, hi - lo], F32, name=f"total{lo}", align_bytes=LINE)
             nc.vector.tensor_tensor(total[:], products[lo][:, 0, :], products[lo][:, 1, :], ADD)
             nc.sync.dma_start(out[:, lo:hi], total[:])
 

from contextlib import ExitStack

import concourse.mybir as mybir
from concourse.masks import make_identity

F32 = mybir.dt.float32
BF16 = mybir.dt.bfloat16
I32 = mybir.dt.int32
U32 = mybir.dt.uint32
U16 = mybir.dt.uint16
U8 = mybir.dt.uint8
FP8X4 = mybir.dt.float8_e4m3fn_x4
FP4X4 = mybir.dt.float4_e2m1fn_x4
COPY = mybir.ActivationFunctionType.Copy
MULT = mybir.AluOpType.mult
ADD = mybir.AluOpType.add

P = 128
K, T, E, C, N = 2560, 768, 12, 128, 128
S = E * C
PASSES = K // 512
FP8_PASSES = 2
FP4_PASSES = PASSES - FP8_PASSES
FLOPS = 2 * K * N * S
LINE = 256

ORDER = (2, 3, 4, 0, 1)
ROW = {2: 0, 3: 0, 4: 12, 0: 4, 1: 8}
FP8_SCALE_ROW = 8
MOVED_PASS = 4
MOVED_ROWS = 100
LAST_QUADRANT = 96
JOINED = 10
SPARE = 112

HALF = 512
HALVES = ((0, HALF), (HALF, T))
WHOLE = ((0, T),)
EVEN = ((0, T // 2), (T // 2, T))
LOADS = (HALVES, EVEN, WHOLE, WHOLE, WHOLE)
VECTOR_CASTS_TO = (320, 640)
LAST_CAST = 16
THIRDS = ((0, HALF), (HALF, 640), (640, T))
PIECES = dict(zip(ORDER, (HALVES, THIRDS, THIRDS, HALVES, THIRDS)))
AHEAD = 6

GROUP = 4
GROUPS = E // GROUP
GROUP_SLOTS = GROUP * C
WIDE = 2048
WIDE_BYTES = 1024
GATE_ROWS = 2 * T // P
SPREAD_BANKS = ("spread0", "spread1", "spread2")
LAST_RUNS = ((8, 10), (10, 11), (11, 12))
OUT_PIECES = ((0, 256, True), (256, 448, False), (448, 640, True), (640, T, True))


def tile_moe_pln_lin_none_kernel(tc, xT, w8_words, w8_scales, w4_words, w4_scales, gate, offs, pos1, pos2, out):
    nc = tc.nc
    first, second, third, fourth, last = ORDER
    with ExitStack() as ctx:
        keep = ctx.enter_context(tc.tile_pool(name="keep", bufs=1))
        psum = ctx.enter_context(tc.psum_pool(name="psum", bufs=1))

        offs_t = keep.tile([P, S // 16], U16, name="offs_t", align_bytes=LINE)
        pos1_t = keep.tile([P, T // 16], U16, name="pos1_t", align_bytes=LINE)
        pos2_t = keep.tile([P, T // 16], U16, name="pos2_t", align_bytes=LINE)

        first_plane = keep.tile([P, WIDE_BYTES], U8, name="first_plane", align_bytes=LINE)
        planes = keep.tile([P, T], U8, name="planes", tag="planes", align_bytes=LINE)
        moved = keep.tile([P, S], U8, name="moved", align_bytes=LINE)
        moved_first = keep.tile([P, JOINED * C], U8, name="moved_first", align_bytes=LINE)
        joined = keep.tile([P, WIDE_BYTES], U8, name="joined", align_bytes=LINE)
        for t in (first_plane[:], planes[:], moved_first[:], joined[:, T:]):
            nc.vector.memset(t.bitcast(I32), 0)
        all_codes = keep.tile([P, (PASSES - 1) * T + WIDE], U32, name="all_codes", align_bytes=LINE)
        nc.vector.memset(all_codes[:, PASSES * T :].bitcast(I32), 0)
        nc.vector.memset(moved[LAST_QUADRANT:P, :].bitcast(I32), 0)

        x_view = xT.rearrange("(a p j) t -> a p j t", p=P, j=4)
        raw = {}

        def load_pass(a):
            raw[a] = []
            for lo, hi in LOADS[ORDER.index(a)]:
                part = keep.tile([P, 4, hi - lo], F32, name=f"raw{a}_{lo}", tag=f"raw{a}_{lo}", align_bytes=LINE)
                nc.sync.dma_start(part[:], x_view[a][:, :, lo:hi])
                raw[a].append((lo, hi, part))

        load_pass(first)
        nc.sync.dma_start(offs_t[:], offs)
        load_pass(second)
        load_pass(third)

        identity = keep.tile([P, P], F32, name="identity")
        make_identity(nc, identity[:])
        gate_rows = keep.tile([P, P], F32, name="gate_rows", align_bytes=LINE)
        nc.gpsimd.memset(gate_rows[:], 0.0)
        both = gate.rearrange("c r (m n) -> (c r m) n", n=P)
        nc.sync.dma_start(gate_rows[:GATE_ROWS, :], both[(N - 1) * T // P : (N + 1) * T // P, :])


        w_views = {
            FP8_PASSES: w8_words.rearrange("e a p n r -> p (e a) (n r)"),
            FP4_PASSES: w4_words.rearrange("e a p b -> p (e a) b"),
        }
        weights = {}

        def load_weights(a, lo, hi):
            passes, index, width = (FP8_PASSES, a, 4 * N) if a < FP8_PASSES else (FP4_PASSES, a - FP8_PASSES, 2 * N)
            tile = keep.tile([P, hi - lo, width], U8, name=f"weights{a}_{lo}", align_bytes=LINE)
            nc.sync.dma_start(tile[:].bitcast(I32), w_views[passes][:, lo * passes + index : hi * passes : passes, :].bitcast(I32))
            for e in range(lo, hi):
                weights[a, e] = tile[:, e - lo, :]

        def load_both_passes(lo, hi):
            tile = keep.tile([P, (hi - lo) * FP8_PASSES, 4 * N], U8, name=f"both_passes{lo}", align_bytes=LINE)
            nc.sync.dma_start(tile[:].bitcast(I32), w_views[FP8_PASSES][:, lo * FP8_PASSES : hi * FP8_PASSES, :].bitcast(I32))
            for e in range(lo, hi):
                for a in (fourth, last):
                    weights[a, e] = tile[:, (e - lo) * FP8_PASSES + a, :]

        def load_scales(rows):
            for r in rows:
                for scales, source, row in ((w4s, w4_scales, 0), (w8s, w8_scales, FP8_SCALE_ROW)):
                    nc.sync.dma_start(scales[row + r : P : 32, :, :N].bitcast(I32), source[:, :, r:16:4, :].rearrange("e a q n -> q (e a) n").bitcast(I32))

        grouped = {
            (a, lo): keep.tile([P, hi - lo, 4], BF16, name=f"grouped{a}_{lo}", tag=f"grouped{a}_{lo}", align_bytes=LINE)
            for a in ORDER
            for lo, hi in PIECES[a]
        }
        base_of = {a: (PASSES - 1 - i) * T for i, a in enumerate(ORDER)}
        codes = {a: all_codes[:, base_of[a] : base_of[a] + T] for a in ORDER}
        wide = {a: all_codes[:, base_of[a] : base_of[a] + WIDE] for a in ORDER}

        def cast(a, lo, hi, on_vector=False):
            piece = max(start for start, end in PIECES[a] if start <= lo)
            for base, end, part in raw[a]:
                start, stop = max(lo, base), min(hi, end)
                if start < stop:
                    dst = grouped[a, piece][:, start - piece : stop - piece, :].rearrange("p (c i) j -> p c j i", i=4)
                    src = part[:, :, start - base : stop - base].rearrange("p j (c i) -> p c j i", i=4)
                    if on_vector:
                        nc.vector.tensor_copy(dst, src)
                    else:
                        nc.scalar.activation(dst, src, COPY)

        def quantise(a, lo, hi):
            plane = first_plane if a == first else planes
            nc.vector.quantize_mx(
                out=codes[a][:, lo:hi].bitcast(FP8X4),
                scales=plane[ROW[a] : P, lo:hi],
                in_=grouped[a, lo][:].rearrange("p t j -> p (t j)"),
            )

        def prepare(a):
            *lead, (lo, hi), final = PIECES[a]
            for piece in lead:
                cast(a, *piece)
                quantise(a, *piece)
            for piece in ((lo, hi - LAST_CAST), final, (hi - LAST_CAST, hi)):
                cast(a, *piece)
            for piece in (final, (lo, hi)):
                quantise(a, *piece)

        def gather(dst, window, lo, hi):
            nc.vector.tensor_copy(dst, window.indirect(offs_t[:, lo // 16 : hi // 16]))

        slots = {}

        def name_slots(what, tile, lo, hi):
            for e in range(lo, hi):
                slots[what, e] = tile[:, (e - lo) * C : (e - lo + 1) * C]

        def gather_run(what, window, dtype, lo, hi, behind=None):
            tag = f"{what}_{lo}" if behind is None else f"grouped{behind}_{PIECES[behind][-1][0]}"
            tile = keep.tile([P, (hi - lo) * C], dtype, name=f"{what}_{lo}", tag=tag, align_bytes=LINE)
            gather(tile[:], window, lo * C, hi * C)
            name_slots(what, tile, lo, hi)

        for (lo, hi), mark in zip(HALVES, VECTOR_CASTS_TO):
            cast(first, lo, mark, on_vector=True)
            cast(first, mark, hi)
            quantise(first, lo, hi)
        gather_run(f"words{first}", wide[first], U32, 0, E)
        for q in range(4):
            nc.sync.dma_start(joined[SPARE + 4 * q : SPARE + 4 * q + 4, :T].bitcast(I32), first_plane[32 * q : 32 * q + 4, :T].bitcast(I32))
        load_pass(fourth)
        load_pass(last)
        w4s = keep.tile([P, E * FP4_PASSES, LINE], U8, name="w4s", tag=f"raw{third}_0", align_bytes=LINE)
        w8s = keep.tile([P, E * FP8_PASSES, LINE], U8, name="w8s", tag=f"raw{second}_0", align_bytes=LINE)
        load_weights(first, 0, E)
        load_scales((0, 1))
        load_weights(second, 0, E)
        load_scales((2, 3))
        load_weights(fourth, 0, E - GROUP)
        load_weights(last, 0, E - GROUP)
        load_weights(third, 0, E)
        load_both_passes(E - GROUP, E - 2)
        gather_run("first_bytes", first_plane[:], U8, JOINED, E - 1)
        prepare(second)
        gather_run("first_bytes", first_plane[:], U8, E - 1, E, behind=second)
        for a, following in ((second, third), (third, fourth)):
            gather_run(f"words{a}", wide[a], U32, 0, E - 1)
            prepare(following)
            gather_run(f"words{a}", codes[a], U32, E - 1, E, behind=following)
        gather_run(f"words{fourth}", wide[fourth], U32, 0, AHEAD)
        prepare(last)
        gather_run(f"words{fourth}", codes[fourth], U32, AHEAD, AHEAD + 1, behind=last)
        turned = psum.tile([P, P], F32, name="turned", tag="turned")
        nc.tensor.transpose(turned[:], gate_rows[:], identity[:])
        gate_columns = keep.tile([P, GATE_ROWS], F32, name="gate_columns", tag=f"raw{last}_0", align_bytes=LINE)
        nc.scalar.copy(gate_columns[:], turned[:, :GATE_ROWS])
        gate_t = keep.tile([P, 2, T], F32, name="gate_t")
        for b, tag in enumerate(SPREAD_BANKS):
            bank = psum.tile([P, GROUP, P], F32, name=f"spread{b}", tag=tag)
            for m in range(GROUP):
                column = gate_columns[:, GROUP * b + m : GROUP * b + m + 1]
                nc.tensor.transpose(bank[:, m, :], column.to_broadcast([P, P]), identity[:])
            nc.scalar.copy(gate_t[:].rearrange("p c t -> p (c t)")[:, b * GROUP * P : (b + 1) * GROUP * P], bank[:].rearrange("p m n -> p (m n)"))
        nc.vector.tensor_copy(joined[:SPARE, :T].bitcast(I32), planes[:SPARE, :].bitcast(I32))

        between = keep.tile([P, C], U32, name="between", tag=f"grouped{last}_{HALF}", align_bytes=LINE)
        gather(between[:], codes[fourth], (AHEAD + 1) * C, (AHEAD + 2) * C)
        name_slots(f"words{fourth}", between, AHEAD + 1, AHEAD + 2)
        got = keep.tile([P, S], U8, name="got", align_bytes=LINE)
        for lo, hi in ((0, JOINED * C // 2), (JOINED * C // 2, JOINED * C), (JOINED * C, S)):
            gather(got[:, lo:hi], joined[:], lo, hi)
        late_words = keep.tile([P, (2 * E - AHEAD - 2) * C], U32, name="late_words", tag="planes", align_bytes=LINE)
        name_slots(f"words{last}", late_words, 0, E)
        name_slots(f"words{fourth}", late_words[:, S:], AHEAD + 2, E)

        def gather_late(a, lo, hi):
            base = 0 if a == last else E - AHEAD - 2
            gather(late_words[:, (base + lo) * C : (base + hi) * C], codes[a], lo * C, hi * C)

        def move_up(lo, hi):
            nc.sync.dma_start(moved[:MOVED_ROWS, lo:hi].bitcast(I32), got[ROW[MOVED_PASS] : ROW[MOVED_PASS] + MOVED_ROWS, lo:hi].bitcast(I32))

        for q in range(4):
            nc.sync.dma_start(moved_first[32 * q : 32 * q + 4, :].bitcast(I32), got[SPARE + 4 * q : SPARE + 4 * q + 4, : JOINED * C].bitcast(I32))
        name_slots("first_bytes", moved_first, 0, JOINED)
        move_up(0, JOINED * C)
        load_both_passes(E - 2, E)
        move_up(JOINED * C, S)
        for tile, source in ((pos1_t, pos1), (pos2_t, pos2)):
            nc.sync.dma_start(tile[:], source)

        y = keep.tile([P, S], F32, name="y")
        pairs = [psum.tile([N, 2 * C], F32, name=f"pair{b}", tag=tag) for b, tag in enumerate(("turned", *SPREAD_BANKS))]
        sums = {e: pairs[e // 2][:, e % 2 * C : (e % 2 + 1) * C] for e in range(E - GROUP)}
        sums.update({e: psum.tile([N, C], F32, name=f"sum{e}")[:] for e in range(E - GROUP, E)})

        done = {}

        def multiply(a, experts):
            for e in experts:
                alone = e >= E - GROUP
                bank = e if alone else e // 2
                done[bank] = done.get(bank, 0) + 1
                if a < FP8_PASSES:
                    lhsT = weights[a, e].bitcast(FP8X4)
                    lhsT_scale = w8s[FP8_SCALE_ROW:P, e * FP8_PASSES + a, :N]
                else:
                    lhsT = weights[a, e].bitcast(FP4X4)
                    lhsT_scale = w4s[:, e * FP4_PASSES + a - FP8_PASSES, :N]
                if a == first:
                    rhs_scale = slots["first_bytes", e]
                elif a == MOVED_PASS:
                    rhs_scale = moved[:, e * C : (e + 1) * C]
                else:
                    rhs_scale = got[ROW[a] : P, e * C : (e + 1) * C]
                nc.tensor.matmul_mx(
                    out=sums[e], lhsT=lhsT, lhsT_scale=lhsT_scale,
                    rhs=slots[f"words{a}", e].bitcast(FP8X4), rhs_scale=rhs_scale,
                    start=done[bank] == 1, stop=done[bank] == PASSES * (1 if alone else 2),
                )

        def empty(e, on_vector=False):
            dst = y[:, e * C : (e + 1) * C]
            if on_vector:
                nc.vector.tensor_copy(dst, sums[e])
            else:
                nc.scalar.copy(dst, sums[e])

        def empty_pair(b):
            nc.scalar.copy(y[:, 2 * b * C : 2 * (b + 1) * C], pairs[b][:])

        group_a, group_b, group_c = (range(g * GROUP, (g + 1) * GROUP) for g in range(GROUPS))
        multiply(first, range(JOINED, E))
        multiply(second, group_a)
        multiply(fourth, group_a)
        multiply(second, group_b)
        multiply(second, group_c)
        multiply(fourth, group_b)
        gather_late(last, 0, GROUP)
        multiply(last, group_a)
        multiply(first, range(JOINED))
        gather_late(last, GROUP, 2 * GROUP)
        multiply(last, group_b)
        gather_late(fourth, AHEAD + 2, E)
        for b in range(len(pairs)):
            multiply(third, range(2 * b, 2 * b + 2))
            empty_pair(b)
        for lo, hi in LAST_RUNS:
            gather_late(last, lo, hi)
            for a in (third, fourth, last):
                multiply(a, range(lo, hi))
            for e in range(lo, hi):
                empty(e, on_vector=(e == E - 2))

        pos_t = (pos1_t, pos2_t)
        fetched, products = {}, {}
        for lo, hi, fused in OUT_PIECES:
            fetched[lo] = keep.tile([P, 1 if fused else 2, hi - lo], F32, name=f"fetched{lo}")
            products[lo] = keep.tile([P, 2, hi - lo], F32, name=f"products{lo}")
            for j, choice in enumerate((1,) if fused else (0, 1)):
                nc.scalar.activation(fetched[lo][:, j, :], y[:].indirect(pos_t[choice][:, lo // 16 : hi // 16]), COPY)

        def fetch_first(lo, hi, fused):
            nc.vector.tensor_tensor(products[lo][:, 0, :], y[:].indirect(pos1_t[:, lo // 16 : hi // 16]), gate_t[:, 0, lo:hi], MULT)

        def weigh(lo, hi, fused):
            choices = slice(1, 2) if fused else slice(0, 2)
            nc.vector.tensor_tensor(products[lo][:, choices, :], fetched[lo][:], gate_t[:, choices, lo:hi], MULT)

        def finish(lo, hi, fused):
            total = keep.tile([P, hi - lo], F32, name=f"total{lo}", align_bytes=LINE)
            nc.vector.tensor_tensor(total[:], products[lo][:, 0, :], products[lo][:, 1, :], ADD)
            nc.sync.dma_start(out[:, lo:hi], total[:])

        piece_a, piece_b, piece_c, piece_d = OUT_PIECES
        fetch_first(*piece_a)
        fetch_first(*piece_c)
        weigh(*piece_a)
        fetch_first(*piece_d)
        finish(*piece_a)
        weigh(*piece_b)
        weigh(*piece_c)
        finish(*piece_b)
        weigh(*piece_d)
        finish(*piece_c)
        finish(*piece_d)
